import numpy as np
import ml_dtypes


def mxq(x, axis, fmt="e4m3"):
    dtype, down = {"e4m3": (ml_dtypes.float8_e4m3fn, 7), "e5m2": (ml_dtypes.float8_e5m2, 14)}[fmt]
    v = np.moveaxis(np.asarray(x, np.float32).astype(ml_dtypes.bfloat16).astype(np.float64), axis, -1)
    blocks = v.reshape(v.shape[:-1] + (-1, 32))
    amax = np.abs(blocks).max(-1, keepdims=True)
    byte = np.maximum(np.where(amax > 0, np.frexp(amax)[1] - 1 + 127, 0) - down, 1)
    scale = np.exp2(byte - 127.0)
    codes = (blocks / scale).astype(np.float32).astype(dtype).astype(np.float64)
    return np.moveaxis((codes * scale).reshape(v.shape), -1, axis)


WIDE = False


def mx_kscale(k):
    if not WIDE:
        return np.ones(k)
    levels = np.array([18, -18])
    if k % 512:
        return np.exp2(np.random.permutation(np.resize(levels, k // 32))).repeat(32)
    a = np.empty((k // 512, 16))
    for p in range(k // 512):
        a[p, :8] = np.random.permutation(np.resize(levels, 8))
        for g in range(8):
            far = levels[np.abs(levels - a[p, g]) >= 10]
            a[p, g + 8] = far[np.random.randint(len(far))]
    return np.exp2(a.ravel()).repeat(32)


def f64(x):
    return np.asarray(x).astype(np.float64)


def striped(idx):
    return np.tile(np.asarray(idx).reshape(-1, 16).T, (8, 1)).astype(np.uint16)


def unstriped(offs):
    return offs[:16].T.reshape(-1).astype(np.int64)


B, N, T, D, DV = 1, 1024, 2048, 512, 512


def setup_inputs():
    n = np.random.standard_normal
    idx = np.random.permutation(T)[:B * N]
    u = np.ones(T)
    u[idx] = mx_kscale(B * N)
    coarse = lambda x: x.astype(np.float32).astype(ml_dtypes.bfloat16).astype(np.float64)
    r = np.random.randint(8, 33, T) / 16.0 * u
    return {
        "xT": (n((D, T)) / np.sqrt(N) / u).astype(np.float32),
        "dyT": (coarse(n((DV, T)))).astype(np.float32),
        "hT": (np.random.randint(-15, 16, (DV, T)) / 16.0).astype(np.float32),
        "ts": np.tile(r, (128, 1)).astype(np.float32),
        "offs": striped(idx),
    }


def reference(xT, dyT, hT, ts, offs):
    idx = unstriped(offs)
    pick = lambda x: x[:, idx].reshape(x.shape[0], B, N).transpose(1, 0, 2)
    h = pick(f64(hT))
    dz = pick(f64(ts))[:, :1, :] * pick(f64(dyT)) * (1.0 - h * h)
    gw = mxq(pick(f64(xT)), 2, "e4m3") @ mxq(dz, 2, "e5m2").transpose(0, 2, 1)
    return gw

@@ -1,0 +1,227 @@
+from contextlib import ExitStack
+
+import concourse.mybir as mybir
+from concourse.masks import make_identity
+
+F32 = mybir.dt.float32
+BF16 = mybir.dt.bfloat16
+U32 = mybir.dt.uint32
+U16 = mybir.dt.uint16
+U8 = mybir.dt.uint8
+E4M3 = mybir.dt.float8_e4m3fn_x4
+E5M2 = mybir.dt.float8_e5m2_x4
+ACT = mybir.ActivationFunctionType
+ALU = mybir.AluOpType
+
+P = 128
+TOKENS = 2048
+SLOTS = 1024
+D = 512
+DV = 512
+PACK = 4
+PASS = P * PACK
+PASSES = SLOTS // PASS
+BLOCKS = D // P
+LIST_COLS = PASS // 16
+
+FLOPS = 2 * D * DV * SLOTS
+
+
+def tile_attend_gex_tnh_w_kernel(tc, xT, dyT, hT, ts, offs, out):
+    nc = tc.nc
+    with ExitStack() as ctx:
+        keep = ctx.enter_context(tc.tile_pool(name="keep", bufs=1))
+        work = ctx.enter_context(tc.tile_pool(name="work", bufs=4))
+        psum = ctx.enter_context(tc.psum_pool(name="psum", bufs=2))
+
+        offsets = keep.tile([P, SLOTS // 16], U16, name="offsets")
+        ts_cols = keep.tile([P, TOKENS // P], F32, name="ts_cols")
+        nc.sync.dma_start(ts_cols[:], ts[0, :].rearrange("(p j) -> p j", p=P))
+        nc.sync.dma_start(offsets[:], offs)
+        lists = [offsets[:, g * LIST_COLS : (g + 1) * LIST_COLS] for g in range(PASSES)]
+        spans = [slice(g * PASS, (g + 1) * PASS) for g in range(PASSES)]
+
+        ident = keep.tile([P, P], F32, name="ident")
+        make_identity(nc, ident[:])
+
+        def chained(b, shape, dtype):
+            return keep.tile(shape, dtype, name="chain%d" % b)
+
+        h_win = [chained(b, [P, TOKENS], F32) for b in range(BLOCKS)]
+        dy_win = [keep.tile([P, TOKENS], F32, name="dy_win%d" % b) for b in range(BLOCKS)]
+        x_raw = [keep.tile([P, TOKENS], F32, name="x_raw%d" % b) for b in range(BLOCKS)]
+        halves = [slice(0, TOKENS // 2), slice(TOKENS // 2, TOKENS)]
+
+        def load(kind, b):
+            rows = slice(b * P, (b + 1) * P)
+            if kind == "h":
+                nc.sync.dma_start(h_win[b][:], hT[rows, :])
+            elif kind == "dy":
+                nc.sync.dma_start(dy_win[b][:], dyT[rows, :])
+            else:
+                for cols in halves:
+                    nc.sync.dma_start(x_raw[b][:, cols], xT[rows, cols])
+
+        for kind, b in [("h", 0), ("x", 0), ("dy", 0), ("h", 1), ("x", 1), ("dy", 1), ("h", 2), ("x", 2), ("dy", 2), ("h", 3), ("x", 3), ("dy", 3)]:
+            load(kind, b)
+
+        ts_win = keep.tile([P, TOKENS], F32, name="ts_win")
+        ts_view = ts_win[:].rearrange("m (p j) -> m p j", p=P)
+        for c in range(TOKENS // PASS):
+            spread = psum.tile([P, PACK, P], F32, name="acc", bufs=4)
+            for j in range(PACK):
+                col = PACK * c + j
+                nc.tensor.transpose(spread[:, j, :], ts_cols[:, col : col + 1].to_broadcast([P, P]), ident[:])
+            nc.vector.tensor_copy(ts_view[:, :, PACK * c : PACK * (c + 1)], spread[:].rearrange("m j p -> m p j"))
+
+        ts_got = keep.tile([P, SLOTS], F32, name="ts_got")
+        dz_codes = keep.tile([P, PASSES, DV], U32, name="dz_codes", align_bytes=64)
+        dz_scales = keep.tile([P, PASSES, DV], U8, name="dz_scales", align_bytes=64)
+        x_codes = keep.tile([P, BLOCKS, PASSES * P], U32, name="x_codes", align_bytes=64)
+        x_scales = keep.tile([P, BLOCKS, PASSES * P], U8, name="x_scales", align_bytes=64)
+        h_got = {}
+        squares = {}
+        dy_ts = {}
+        dz_banks = {}
+        dz_turned = {}
+        x_win = {}
+        x_turned = {}
+        x_banks = {}
+
+        def gather_ts():
+            nc.vector.tensor_copy(ts_got[:], ts_win[:].indirect(offsets[:]))
+
+        def gather_h(b):
+            if b == 0:
+                h_got[b] = keep.tile([P, SLOTS], F32, name="h_got0")
+            else:
+                h_got[b] = chained(b - 1, [P, SLOTS], F32)
+            for g in range(PASSES):
+                nc.vector.tensor_copy(h_got[b][:, spans[g]], h_win[b][:].indirect(lists[g]))
+                h_sq = work.tile([P, PASS], F32, name="h_sq")
+                nc.scalar.activation(h_sq[:], h_got[b][:, spans[g]], ACT.Square)
+                squares[b, g] = h_sq
+
+        def gather_dy(b, g):
+            if g == 0:
+                dy_ts[b] = chained(b, [P, SLOTS], F32)
+            nc.vector.tensor_tensor(
+                dy_ts[b][:, spans[g]], dy_win[b][:].indirect(lists[g]), ts_got[:, spans[g]], ALU.mult
+            )
+
+        def form_dz(b, g):
+            neg_dz = work.tile([P, PASS], BF16, name="neg_dz")
+            nc.vector.scalar_tensor_tensor(
+                neg_dz[:], squares[b, g][:], 1.0, dy_ts[b][:, spans[g]], ALU.subtract, ALU.mult
+            )
+            pairs = neg_dz[:].bitcast(F32).rearrange("n (p u) -> n u p", u=2)
+            bank = psum.tile([P, 2, P], F32, name="dz_bank")
+            for u in range(2):
+                nc.tensor.transpose(bank[:, u, :], pairs[:, u, :], ident[:])
+            dz_banks[b, g] = bank
+
+        def fetch_dz(b, g):
+            turned = work.tile([P, PASS], BF16, name="dz_turned", align_bytes=64)
+            words = turned[:].bitcast(F32).rearrange("p (n u) -> p n u", u=2)
+            source = dz_banks[b, g][:].rearrange("p u n -> p n u")
+            if b == BLOCKS - 1:
+                nc.vector.tensor_copy(words, source)
+            else:
+                nc.scalar.copy(words, source)
+            dz_turned[b, g] = turned
+
+        def quantize_dz(b, g):
+            cols = slice(b * P, (b + 1) * P)
+            nc.vector.quantize_mx(
+                out=dz_codes[:, g, cols].bitcast(E5M2), scales=dz_scales[:, g, cols], in_=dz_turned[b, g][:]
+            )
+
+        def cast_x(b, half):
+            if half == 0:
+                x_win[b] = keep.tile([P, TOKENS], BF16, name="x_win")
+            nc.scalar.activation(x_win[b][:, halves[half]], x_raw[b][:, halves[half]], ACT.Copy)
+
+        def gather_x(b):
+            bank = psum.tile([P, PASSES, 2, P], F32, name="x_bank")
+            if b == 0:
+                x_got = keep.tile([P, PASSES, 2, P, 2], BF16, name="x_got0")
+            else:
+                x_got = chained(b - 1, [P, PASSES, 2, P, 2], BF16)
+            for g in range(PASSES):
+                nc.scalar.activation(
+                    x_got[:, g].rearrange("q u p e -> q p u e"), x_win[b][:].indirect(lists[g]), ACT.Copy
+                )
+                pairs = x_got[:, g].rearrange("q u p e -> q (u p e)").bitcast(F32)
+                for u in range(2):
+                    nc.tensor.transpose(bank[:, g, u, :], pairs[:, u * P : (u + 1) * P], ident[:])
+            x_banks[b] = bank
+
+        def fetch_x(b):
+            bank = x_banks[b]
+            turned = work.tile([P, PASSES * PASS], BF16, name="x_turned", align_bytes=64)
+            nc.scalar.copy(
+                turned[:].bitcast(F32).rearrange("p (g d u) -> p g d u", g=PASSES, u=2),
+                bank[:].rearrange("p g u d -> p g d u"),
+            )
+            x_turned[b] = turned
+
+        def quantize_x(b):
+            nc.vector.quantize_mx(out=x_codes[:, b, :].bitcast(E4M3), scales=x_scales[:, b, :], in_=x_turned[b][:])
+
+        last = BLOCKS - 1
+        for b in range(BLOCKS):
+            gather_h(b)
+            if b == 0:
+                gather_ts()
+                cast_x(0, 0)
+                cast_x(0, 1)
+            else:
+                quantize_x(b - 1)
+                for g in range(PASSES):
+                    quantize_dz(b - 1, g)
+            gather_x(b)
+            if b < last:
+                cast_x(b + 1, 0)
+                fetch_x(b)
+                for g in range(PASSES):
+                    gather_dy(b, g)
+                for g in range(PASSES):
+                    form_dz(b, g)
+                for g in range(PASSES):
+                    fetch_dz(b, g)
+                cast_x(b + 1, 1)
+        fetch_x(last)
+        gather_dy(last, 0)
+        form_dz(last, 0)
+        gather_dy(last, 1)
+        fetch_dz(last, 0)
+        form_dz(last, 1)
+        quantize_dz(last, 0)
+        quantize_x(last)
+        fetch_dz(last, 1)
+        quantize_dz(last, 1)
+
+        accs = [psum.tile([P, DV], F32, name="acc", bufs=4) for b in range(BLOCKS)]
+
+        def multiply(b, g):
+            cols = slice(g * P, (g + 1) * P)
+            nc.tensor.matmul_mx(
+                out=accs[b][:],
+                lhsT=x_codes[:, b, cols].bitcast(E4M3),
+                lhsT_scale=x_scales[:, b, cols],
+                rhs=dz_codes[:, g, :].bitcast(E5M2),
+                rhs_scale=dz_scales[:, g, :],
+                start=(g == 0),
+                stop=(g == PASSES - 1),
+            )
+
+        for g in range(PASSES):
+            for b in range(BLOCKS):
+                multiply(b, g)
+        for b in range(BLOCKS):
+            result = work.tile([P, DV], F32, name="result")
+            if b % 2 == 0:
+                nc.vector.tensor_scalar_mul(result[:], accs[b][:], -1.0)
+            else:
+                nc.scalar.activation(result[:], accs[b][:], ACT.Copy, scale=-1.0)
+            nc.sync.dma_start(out[0, b * P : (b + 1) * P, :], result[:])

@@ -32,22 +32,21 @@ def tile_attend_gex_tnh_w_kernel(tc, xT, dyT, hT, ts, offs, out):
     with ExitStack() as ctx:
         keep = ctx.enter_context(tc.tile_pool(name="keep", bufs=1))
         work = ctx.enter_context(tc.tile_pool(name="work", bufs=4))
-        psum = ctx.enter_context(tc.psum_pool(name="psum", bufs=2))
+        psum = ctx.enter_context(tc.psum_pool(name="psum", bufs=1))
+
+        def tenant(slot, shape, dtype):
+            return keep.tile(shape, dtype, name=slot, align_bytes=64)
 
         offsets = keep.tile([P, SLOTS // 16], U16, name="offsets")
-        ts_cols = keep.tile([P, TOKENS // P], F32, name="ts_cols")
+        ts_cols = tenant("first", [P, TOKENS // P], F32)
         nc.sync.dma_start(ts_cols[:], ts[0, :].rearrange("(p j) -> p j", p=P))
-        nc.sync.dma_start(offsets[:], offs)
         lists = [offsets[:, g * LIST_COLS : (g + 1) * LIST_COLS] for g in range(PASSES)]
         spans = [slice(g * PASS, (g + 1) * PASS) for g in range(PASSES)]
 
         ident = keep.tile([P, P], F32, name="ident")
         make_identity(nc, ident[:])
 
-        def chained(b, shape, dtype):
-            return keep.tile(shape, dtype, name="chain%d" % b)
-
-        h_win = [chained(b, [P, TOKENS], F32) for b in range(BLOCKS)]
+        h_win = [keep.tile([P, TOKENS], F32, name="h_win%d" % b) for b in range(BLOCKS)]
         dy_win = [keep.tile([P, TOKENS], F32, name="dy_win%d" % b) for b in range(BLOCKS)]
         x_raw = [keep.tile([P, TOKENS], F32, name="x_raw%d" % b) for b in range(BLOCKS)]
         halves = [slice(0, TOKENS // 2), slice(TOKENS // 2, TOKENS)]
@@ -62,8 +61,10 @@ def tile_attend_gex_tnh_w_kernel(tc, xT, dyT, hT, ts, offs, out):
                 for cols in halves:
                     nc.sync.dma_start(x_raw[b][:, cols], xT[rows, cols])
 
-        for kind, b in [("h", 0), ("x", 0), ("dy", 0), ("h", 1), ("x", 1), ("dy", 1), ("h", 2), ("x", 2), ("dy", 2), ("h", 3), ("x", 3), ("dy", 3)]:
+        for kind, b in [("h", 0), ("x", 0), ("x", 1), ("dy", 0), ("h", 1), ("x", 2), ("dy", 1), ("h", 2), ("x", 3), ("dy", 2), ("h", 3), ("dy", 3)]:
             load(kind, b)
+            if (kind, b) == ("h", 0):
+                nc.sync.dma_start(offsets[:], offs)
 
         ts_win = keep.tile([P, TOKENS], F32, name="ts_win")
         ts_view = ts_win[:].rearrange("m (p j) -> m p j", p=P)
@@ -75,131 +76,116 @@ def tile_attend_gex_tnh_w_kernel(tc, xT, dyT, hT, ts, offs, out):
             nc.vector.tensor_copy(ts_view[:, :, PACK * c : PACK * (c + 1)], spread[:].rearrange("m j p -> m p j"))
 
         ts_got = keep.tile([P, SLOTS], F32, name="ts_got")
-        dz_codes = keep.tile([P, PASSES, DV], U32, name="dz_codes", align_bytes=64)
-        dz_scales = keep.tile([P, PASSES, DV], U8, name="dz_scales", align_bytes=64)
-        x_codes = keep.tile([P, BLOCKS, PASSES * P], U32, name="x_codes", align_bytes=64)
-        x_scales = keep.tile([P, BLOCKS, PASSES * P], U8, name="x_scales", align_bytes=64)
+        dz_codes = {}
+        dz_scales = [keep.tile([P, DV], U8, name="dz_scales%d" % g, align_bytes=64) for g in range(PASSES)]
+        x_codes = {}
+        x_scales = [keep.tile([P, PASSES * P], U8, name="x_scales%d" % b, align_bytes=64) for b in range(BLOCKS)]
         h_got = {}
         squares = {}
         dy_ts = {}
         dz_banks = {}
         dz_turned = {}
         x_win = {}
-        x_turned = {}
         x_banks = {}
+        x_turned = {}
+        slot_of = {}
+        fresh = ["s%d" % i for i in range(40)]
+
+        def after(key, previous, shape, dtype):
+            slot_of[key] = slot_of[previous] if previous in slot_of else fresh.pop()
+            return tenant(slot_of[key], shape, dtype)
 
         def gather_ts():
             nc.vector.tensor_copy(ts_got[:], ts_win[:].indirect(offsets[:]))
 
         def gather_h(b):
             if b == 0:
-                h_got[b] = keep.tile([P, SLOTS], F32, name="h_got0")
+                both = tenant("first", [P, SLOTS], F32)
+                h_got[0, 0], h_got[0, 1] = both[:, spans[0]], both[:, spans[1]]
             else:
-                h_got[b] = chained(b - 1, [P, SLOTS], F32)
+                h_got[b, 0] = after(("h", b, 0), ("dy", b - 1, 0), [P, PASS], F32)[:]
+                h_got[b, 1] = after(("h", b, 1), ("sq", b - 1, 0), [P, PASS], F32)[:]
             for g in range(PASSES):
-                nc.vector.tensor_copy(h_got[b][:, spans[g]], h_win[b][:].indirect(lists[g]))
-                h_sq = work.tile([P, PASS], F32, name="h_sq")
-                nc.scalar.activation(h_sq[:], h_got[b][:, spans[g]], ACT.Square)
-                squares[b, g] = h_sq
+                nc.vector.tensor_copy(h_got[b, g], h_win[b][:].indirect(lists[g]))
+
+        def square_h(b, g):
+            squares[b, g] = after(("sq", b, g), None, [P, PASS], F32)
+            nc.scalar.activation(squares[b, g][:], h_got[b, g], ACT.Square)
 
         def gather_dy(b, g):
-            if g == 0:
-                dy_ts[b] = chained(b, [P, SLOTS], F32)
+            previous = ("dy", b - 1, 1) if g == 0 else ("sq", b - 1, 1)
+            dy_ts[b, g] = after(("dy", b, g), previous, [P, PASS], F32)
             nc.vector.tensor_tensor(
-                dy_ts[b][:, spans[g]], dy_win[b][:].indirect(lists[g]), ts_got[:, spans[g]], ALU.mult
+                dy_ts[b, g][:], dy_win[b][:].indirect(lists[g]), ts_got[:, spans[g]], ALU.mult
             )
 
         def form_dz(b, g):
-            neg_dz = work.tile([P, PASS], BF16, name="neg_dz")
+            neg_dz = after(("nz", b, g), None, [P, PASS], BF16)
             nc.vector.scalar_tensor_tensor(
-                neg_dz[:], squares[b, g][:], 1.0, dy_ts[b][:, spans[g]], ALU.subtract, ALU.mult
+                neg_dz[:], squares[b, g][:], 1.0, dy_ts[b, g][:], ALU.subtract, ALU.mult
             )
             pairs = neg_dz[:].bitcast(F32).rearrange("n (p u) -> n u p", u=2)
-            bank = psum.tile([P, 2, P], F32, name="dz_bank")
-            for u in range(2):
-                nc.tensor.transpose(bank[:, u, :], pairs[:, u, :], ident[:])
-            dz_banks[b, g] = bank
-
-        def fetch_dz(b, g):
-            turned = work.tile([P, PASS], BF16, name="dz_turned", align_bytes=64)
-            words = turned[:].bitcast(F32).rearrange("p (n u) -> p n u", u=2)
-            source = dz_banks[b, g][:].rearrange("p u n -> p n u")
             if b == BLOCKS - 1:
-                nc.vector.tensor_copy(words, source)
+                if g == 0:
+                    dz_banks[b, g] = psum.tile([P, 2, P], F32, name="dz_bank", bufs=2)[:]
+                else:
+                    dz_banks[b, g] = psum.tile([P, 2, P], F32, name="dz_bank_last")[:]
+            elif g == 0:
+                dz_banks[b] = psum.tile([P, PASSES, 2, P], F32, name="dz_bank", bufs=2)
+                dz_banks[b, 0], dz_banks[b, 1] = dz_banks[b][:, 0], dz_banks[b][:, 1]
+            for u in range(2):
+                nc.tensor.transpose(dz_banks[b, g][:, u, :], pairs[:, u, :], ident[:])
+
+        def fetch_dz(b):
+            turned = work.tile([P, PASSES, PASS], BF16, name="dz_turned", align_bytes=64)
+            words = turned[:].rearrange("p g k -> p (g k)").bitcast(F32).rearrange("p (g n u) -> p g n u", g=PASSES, u=2)
+            if b < BLOCKS - 1:
+                nc.scalar.copy(words, dz_banks[b][:].rearrange("p g u n -> p g n u"))
             else:
-                nc.scalar.copy(words, source)
-            dz_turned[b, g] = turned
+                for g in range(PASSES):
+                    nc.scalar.copy(words[:, g], dz_banks[b, g].rearrange("p u n -> p n u"))
+            dz_turned[b] = turned
 
         def quantize_dz(b, g):
             cols = slice(b * P, (b + 1) * P)
             nc.vector.quantize_mx(
-                out=dz_codes[:, g, cols].bitcast(E5M2), scales=dz_scales[:, g, cols], in_=dz_turned[b, g][:]
+                out=dz_codes[g][:, cols].bitcast(E5M2), scales=dz_scales[g][:, cols], in_=dz_turned[b][:, g, :]
             )
 
         def cast_x(b, half):
             if half == 0:
-                x_win[b] = keep.tile([P, TOKENS], BF16, name="x_win")
-            nc.scalar.activation(x_win[b][:, halves[half]], x_raw[b][:, halves[half]], ACT.Copy)
+                x_win[b] = keep.tile([P, TOKENS], BF16, name="x_win%d" % b)
+            if b >= 2 and half == 1:
+                nc.vector.tensor_copy(x_win[b][:, halves[half]], x_raw[b][:, halves[half]])
+            else:
+                nc.scalar.activation(x_win[b][:, halves[half]], x_raw[b][:, halves[half]], ACT.Copy)
 
         def gather_x(b):
             bank = psum.tile([P, PASSES, 2, P], F32, name="x_bank")
-            if b == 0:
-                x_got = keep.tile([P, PASSES, 2, P, 2], BF16, name="x_got0")
-            else:
-                x_got = chained(b - 1, [P, PASSES, 2, P, 2], BF16)
+            x_got = after(("xg", b), ("nz", b - 1, 0), [P, 2, PASSES * P, 2], BF16)
+            nc.scalar.activation(
+                x_got[:].rearrange("q u p e -> q p u e"), x_win[b][:].indirect(offsets[:]), ACT.Copy
+            )
+            pairs = x_got[:].rearrange("q u p e -> q (u p e)").bitcast(F32)
             for g in range(PASSES):
-                nc.scalar.activation(
-                    x_got[:, g].rearrange("q u p e -> q p u e"), x_win[b][:].indirect(lists[g]), ACT.Copy
-                )
-                pairs = x_got[:, g].rearrange("q u p e -> q (u p e)").bitcast(F32)
                 for u in range(2):
-                    nc.tensor.transpose(bank[:, g, u, :], pairs[:, u * P : (u + 1) * P], ident[:])
+                    first = (u * PASSES + g) * P
+                    nc.tensor.transpose(bank[:, g, u, :], pairs[:, first : first + P], ident[:])
             x_banks[b] = bank
 
         def fetch_x(b):
-            bank = x_banks[b]
             turned = work.tile([P, PASSES * PASS], BF16, name="x_turned", align_bytes=64)
             nc.scalar.copy(
                 turned[:].bitcast(F32).rearrange("p (g d u) -> p g d u", g=PASSES, u=2),
-                bank[:].rearrange("p g u d -> p g d u"),
+                x_banks[b][:].rearrange("p g u d -> p g d u"),
             )
             x_turned[b] = turned
 
         def quantize_x(b):
-            nc.vector.quantize_mx(out=x_codes[:, b, :].bitcast(E4M3), scales=x_scales[:, b, :], in_=x_turned[b][:])
-
-        last = BLOCKS - 1
-        for b in range(BLOCKS):
-            gather_h(b)
-            if b == 0:
-                gather_ts()
-                cast_x(0, 0)
-                cast_x(0, 1)
-            else:
-                quantize_x(b - 1)
-                for g in range(PASSES):
-                    quantize_dz(b - 1, g)
-            gather_x(b)
-            if b < last:
-                cast_x(b + 1, 0)
-                fetch_x(b)
-                for g in range(PASSES):
-                    gather_dy(b, g)
-                for g in range(PASSES):
-                    form_dz(b, g)
-                for g in range(PASSES):
-                    fetch_dz(b, g)
-                cast_x(b + 1, 1)
-        fetch_x(last)
-        gather_dy(last, 0)
-        form_dz(last, 0)
-        gather_dy(last, 1)
-        fetch_dz(last, 0)
-        form_dz(last, 1)
-        quantize_dz(last, 0)
-        quantize_x(last)
-        fetch_dz(last, 1)
-        quantize_dz(last, 1)
+            if b < 2:
+                pair = after(("xc", b), ("sq", BLOCKS - 1, b), [P, 2, PASSES * P], U32)
+                x_codes[b], x_codes[b + 2] = pair[:, 0, :], pair[:, 1, :]
+            nc.vector.quantize_mx(out=x_codes[b][:, :].bitcast(E4M3), scales=x_scales[b][:, :], in_=x_turned[b][:])
 
         accs = [psum.tile([P, DV], F32, name="acc", bufs=4) for b in range(BLOCKS)]
 
@@ -207,21 +193,49 @@ def tile_attend_gex_tnh_w_kernel(tc, xT, dyT, hT, ts, offs, out):
             cols = slice(g * P, (g + 1) * P)
             nc.tensor.matmul_mx(
                 out=accs[b][:],
-                lhsT=x_codes[:, b, cols].bitcast(E4M3),
-                lhsT_scale=x_scales[:, b, cols],
-                rhs=dz_codes[:, g, :].bitcast(E5M2),
-                rhs_scale=dz_scales[:, g, :],
+                lhsT=x_codes[b][:, cols].bitcast(E4M3),
+                lhsT_scale=x_scales[b][:, cols],
+                rhs=dz_codes[g][:, :].bitcast(E5M2),
+                rhs_scale=dz_scales[g][:, :],
                 start=(g == 0),
                 stop=(g == PASSES - 1),
             )
 
-        for g in range(PASSES):
-            for b in range(BLOCKS):
-                multiply(b, g)
-        for b in range(BLOCKS):
+        def store(b):
             result = work.tile([P, DV], F32, name="result")
             if b % 2 == 0:
-                nc.vector.tensor_scalar_mul(result[:], accs[b][:], -1.0)
-            else:
                 nc.scalar.activation(result[:], accs[b][:], ACT.Copy, scale=-1.0)
+            else:
+                nc.vector.tensor_scalar_mul(result[:], accs[b][:], -1.0)
             nc.sync.dma_start(out[0, b * P : (b + 1) * P, :], result[:])
+
+        last = BLOCKS - 1
+        for b in range(BLOCKS):
+            gather_h(b)
+            if b == 0:
+                gather_ts()
+            else:
+                fetch_dz(b - 1)
+            cast_x(b, 0)
+            cast_x(b, 1)
+            if b > 0:
+                fetch_x(b - 1)
+            square_h(b, 0)
+            gather_x(b)
+            square_h(b, 1)
+            for g in range(PASSES):
+                gather_dy(b, g)
+            for g in range(PASSES):
+                form_dz(b, g)
+        fetch_x(last)
+        for b in range(BLOCKS):
+            quantize_x(b)
+        fetch_dz(last)
+        for g in range(PASSES):
+            dz_codes[g] = after(("dzc", g), ("dy", last, g), [P, DV], U32)
+            for b in range(BLOCKS):
+                quantize_dz(b, g)
+        for b in range(BLOCKS):
+            for g in range(PASSES):
+                multiply(b, g)
+            store(b)

@@ -22,7 +22,16 @@ PACK = 4
 PASS = P * PACK
 PASSES = SLOTS // PASS
 BLOCKS = D // P
+LAST = BLOCKS - 1
 LIST_COLS = PASS // 16
+MX_ALIGN = 64
+
+TS_RUN = TOKENS // P
+TS_HALF = TS_RUN // 2
+BANK_COLS = 4
+
+LOAD_ORDER = [("h", 0), ("x", 0), ("dy", 0)] + [(kind, b) for b in range(1, BLOCKS) for kind in ("x", "h", "dy")]
+CASTS_ON_VECTOR = ((2, 0), (3, 1))
 
 FLOPS = 2 * D * DV * SLOTS
 
@@ -31,101 +40,87 @@ def tile_attend_gex_tnh_w_kernel(tc, xT, dyT, hT, ts, offs, out):
     nc = tc.nc
     with ExitStack() as ctx:
         keep = ctx.enter_context(tc.tile_pool(name="keep", bufs=1))
-        work = ctx.enter_context(tc.tile_pool(name="work", bufs=4))
+        per_block = ctx.enter_context(tc.tile_pool(name="per_block", bufs=BLOCKS))
         psum = ctx.enter_context(tc.psum_pool(name="psum", bufs=1))
 
-        def tenant(slot, shape, dtype):
-            return keep.tile(shape, dtype, name=slot, align_bytes=64)
+        tag_of = {}
+
+        def successor(key, previous, shape, dtype):
+            tag_of[key] = tag_of.get(previous, "-".join(map(str, key)))
+            return keep.tile(shape, dtype, name=tag_of[key], align_bytes=MX_ALIGN)
 
         offsets = keep.tile([P, SLOTS // 16], U16, name="offsets")
-        ts_cols = tenant("first", [P, TOKENS // P], F32)
-        nc.sync.dma_start(ts_cols[:], ts[0, :].rearrange("(p j) -> p j", p=P))
-        lists = [offsets[:, g * LIST_COLS : (g + 1) * LIST_COLS] for g in range(PASSES)]
-        spans = [slice(g * PASS, (g + 1) * PASS) for g in range(PASSES)]
+        ts_runs = ts[0, :].rearrange("(p j) -> p j", p=P)
+        ts_cols = [successor(("ts_cols", i), None, [P, TS_HALF], F32) for i in range(2)]
+        for i in range(2):
+            nc.sync.dma_start(ts_cols[i][:], ts_runs[:, TS_HALF * i : TS_HALF * (i + 1)])
+        pass_lists = [offsets[:, g * LIST_COLS : (g + 1) * LIST_COLS] for g in range(PASSES)]
+        pass_slots = [slice(g * PASS, (g + 1) * PASS) for g in range(PASSES)]
 
         ident = keep.tile([P, P], F32, name="ident")
         make_identity(nc, ident[:])
 
-        h_win = [keep.tile([P, TOKENS], F32, name="h_win%d" % b) for b in range(BLOCKS)]
+        h_win = [successor(("h_win", b), None, [P, TOKENS], F32) for b in range(BLOCKS)]
         dy_win = [keep.tile([P, TOKENS], F32, name="dy_win%d" % b) for b in range(BLOCKS)]
         x_raw = [keep.tile([P, TOKENS], F32, name="x_raw%d" % b) for b in range(BLOCKS)]
-        halves = [slice(0, TOKENS // 2), slice(TOKENS // 2, TOKENS)]
+        token_halves = [slice(0, TOKENS // 2), slice(TOKENS // 2, TOKENS)]
 
-        def load(kind, b):
+        for kind, b in LOAD_ORDER:
             rows = slice(b * P, (b + 1) * P)
             if kind == "h":
                 nc.sync.dma_start(h_win[b][:], hT[rows, :])
             elif kind == "dy":
                 nc.sync.dma_start(dy_win[b][:], dyT[rows, :])
             else:
-                for cols in halves:
+                for cols in token_halves:
                     nc.sync.dma_start(x_raw[b][:, cols], xT[rows, cols])
-
-        for kind, b in [("h", 0), ("x", 0), ("x", 1), ("dy", 0), ("h", 1), ("x", 2), ("dy", 1), ("h", 2), ("x", 3), ("dy", 2), ("h", 3), ("dy", 3)]:
-            load(kind, b)
-            if (kind, b) == ("h", 0):
+            if (kind, b) == LOAD_ORDER[0]:
                 nc.sync.dma_start(offsets[:], offs)
 
         ts_win = keep.tile([P, TOKENS], F32, name="ts_win")
         ts_view = ts_win[:].rearrange("m (p j) -> m p j", p=P)
-        for c in range(TOKENS // PASS):
-            spread = psum.tile([P, PACK, P], F32, name="acc", bufs=4)
-            for j in range(PACK):
-                col = PACK * c + j
-                nc.tensor.transpose(spread[:, j, :], ts_cols[:, col : col + 1].to_broadcast([P, P]), ident[:])
-            nc.vector.tensor_copy(ts_view[:, :, PACK * c : PACK * (c + 1)], spread[:].rearrange("m j p -> m p j"))
+        for c in (0, 2, 1, 3):
+            spread = psum.tile([P, BANK_COLS, P], F32, name="acc", bufs=BLOCKS)
+            for j in range(BANK_COLS):
+                col = BANK_COLS * (c % 2) + j
+                nc.tensor.transpose(spread[:, j, :], ts_cols[c // 2][:, col : col + 1].to_broadcast([P, P]), ident[:])
+            nc.scalar.copy(ts_view[:, :, BANK_COLS * c : BANK_COLS * (c + 1)], spread[:].rearrange("m j p -> m p j"))
 
         ts_got = keep.tile([P, SLOTS], F32, name="ts_got")
-        dz_codes = {}
-        dz_scales = [keep.tile([P, DV], U8, name="dz_scales%d" % g, align_bytes=64) for g in range(PASSES)]
-        x_codes = {}
-        x_scales = [keep.tile([P, PASSES * P], U8, name="x_scales%d" % b, align_bytes=64) for b in range(BLOCKS)]
-        h_got = {}
-        squares = {}
-        dy_ts = {}
-        dz_banks = {}
-        dz_turned = {}
-        x_win = {}
-        x_banks = {}
-        x_turned = {}
-        slot_of = {}
-        fresh = ["s%d" % i for i in range(40)]
-
-        def after(key, previous, shape, dtype):
-            slot_of[key] = slot_of[previous] if previous in slot_of else fresh.pop()
-            return tenant(slot_of[key], shape, dtype)
-
-        def gather_ts():
-            nc.vector.tensor_copy(ts_got[:], ts_win[:].indirect(offsets[:]))
+        dz_scales = [keep.tile([P, DV], U8, name="dz_scales%d" % g, align_bytes=MX_ALIGN) for g in range(PASSES)]
+        x_scales = [keep.tile([P, PASSES * P], U8, name="x_scales%d" % b, align_bytes=MX_ALIGN) for b in range(BLOCKS)]
+        h_got, squares, dy_ts, dz_banks, dz_turned, dz_codes = {}, {}, {}, {}, {}, {}
+        x_win, x_banks, x_turned, x_codes = {}, {}, {}, {}
 
         def gather_h(b):
-            if b == 0:
-                both = tenant("first", [P, SLOTS], F32)
-                h_got[0, 0], h_got[0, 1] = both[:, spans[0]], both[:, spans[1]]
-            else:
-                h_got[b, 0] = after(("h", b, 0), ("dy", b - 1, 0), [P, PASS], F32)[:]
-                h_got[b, 1] = after(("h", b, 1), ("sq", b - 1, 0), [P, PASS], F32)[:]
+            h_got[b, 0] = successor(("h_got", b, 0), ("dy_ts", b - 1, 0), [P, PASS], F32)
+            h_got[b, 1] = successor(("h_got", b, 1), ("squares", b - 1, 0), [P, PASS], F32)
             for g in range(PASSES):
-                nc.vector.tensor_copy(h_got[b, g], h_win[b][:].indirect(lists[g]))
+                nc.vector.tensor_copy(h_got[b, g][:], h_win[b][:].indirect(pass_lists[g]))
 
         def square_h(b, g):
-            squares[b, g] = after(("sq", b, g), None, [P, PASS], F32)
-            nc.scalar.activation(squares[b, g][:], h_got[b, g], ACT.Square)
+            if b > 0:
+                squares[b, g] = successor(("squares", b, g), None, [P, PASS], F32)[:]
+            elif g == 0:
+                both = successor(("squares", 0, 0), ("ts_cols", 0), [P, SLOTS], F32)
+                squares[0, 0], squares[0, 1] = both[:, pass_slots[0]], both[:, pass_slots[1]]
+            nc.scalar.activation(squares[b, g], h_got[b, g][:], ACT.Square)
 
         def gather_dy(b, g):
-            previous = ("dy", b - 1, 1) if g == 0 else ("sq", b - 1, 1)
-            dy_ts[b, g] = after(("dy", b, g), previous, [P, PASS], F32)
+            if g == 0:
+                previous = ("dy_ts", b - 1, 1)
+            else:
+                previous = ("neg_dz", 0, 1) if b == 1 else ("squares", b - 1, 1)
+            dy_ts[b, g] = successor(("dy_ts", b, g), previous, [P, PASS], F32)
             nc.vector.tensor_tensor(
-                dy_ts[b, g][:], dy_win[b][:].indirect(lists[g]), ts_got[:, spans[g]], ALU.mult
+                dy_ts[b, g][:], dy_win[b][:].indirect(pass_lists[g]), ts_got[:, pass_slots[g]], ALU.mult
             )
 
         def form_dz(b, g):
-            neg_dz = after(("nz", b, g), None, [P, PASS], BF16)
-            nc.vector.scalar_tensor_tensor(
-                neg_dz[:], squares[b, g][:], 1.0, dy_ts[b, g][:], ALU.subtract, ALU.mult
-            )
+            neg_dz = successor(("neg_dz", b, g), None, [P, PASS], BF16)
+            nc.vector.scalar_tensor_tensor(neg_dz[:], squares[b, g], 1.0, dy_ts[b, g][:], ALU.subtract, ALU.mult)
             pairs = neg_dz[:].bitcast(F32).rearrange("n (p u) -> n u p", u=2)
-            if b == BLOCKS - 1:
+            if b == LAST:
                 if g == 0:
                     dz_banks[b, g] = psum.tile([P, 2, P], F32, name="dz_bank", bufs=2)[:]
                 else:
@@ -137,14 +132,14 @@ def tile_attend_gex_tnh_w_kernel(tc, xT, dyT, hT, ts, offs, out):
                 nc.tensor.transpose(dz_banks[b, g][:, u, :], pairs[:, u, :], ident[:])
 
         def fetch_dz(b):
-            turned = work.tile([P, PASSES, PASS], BF16, name="dz_turned", align_bytes=64)
-            words = turned[:].rearrange("p g k -> p (g k)").bitcast(F32).rearrange("p (g n u) -> p g n u", g=PASSES, u=2)
-            if b < BLOCKS - 1:
-                nc.scalar.copy(words, dz_banks[b][:].rearrange("p g u n -> p g n u"))
+            dz_turned[b] = per_block.tile([P, PASSES, PASS], BF16, name="dz_turned", align_bytes=MX_ALIGN)
+            pairs = dz_turned[b][:].rearrange("p g k -> p (g k)").bitcast(F32)
+            pairs = pairs.rearrange("p (g n u) -> p g n u", g=PASSES, u=2)
+            if b < LAST:
+                nc.scalar.copy(pairs, dz_banks[b][:].rearrange("p g u n -> p g n u"))
             else:
                 for g in range(PASSES):
-                    nc.scalar.copy(words[:, g], dz_banks[b, g].rearrange("p u n -> p n u"))
-            dz_turned[b] = turned
+                    nc.scalar.copy(pairs[:, g], dz_banks[b, g].rearrange("p u n -> p n u"))
 
         def quantize_dz(b, g):
             cols = slice(b * P, (b + 1) * P)
@@ -154,40 +149,38 @@ def tile_attend_gex_tnh_w_kernel(tc, xT, dyT, hT, ts, offs, out):
 
         def cast_x(b, half):
             if half == 0:
-                x_win[b] = keep.tile([P, TOKENS], BF16, name="x_win%d" % b)
-            if b >= 2 and half == 1:
-                nc.vector.tensor_copy(x_win[b][:, halves[half]], x_raw[b][:, halves[half]])
+                x_win[b] = successor(("x_win", b), ("ts_cols", 1) if b == 0 else None, [P, TOKENS], BF16)
+            cols = token_halves[half]
+            if (b, half) in CASTS_ON_VECTOR:
+                nc.vector.tensor_copy(x_win[b][:, cols], x_raw[b][:, cols])
             else:
-                nc.scalar.activation(x_win[b][:, halves[half]], x_raw[b][:, halves[half]], ACT.Copy)
+                nc.scalar.activation(x_win[b][:, cols], x_raw[b][:, cols], ACT.Copy)
 
         def gather_x(b):
-            bank = psum.tile([P, PASSES, 2, P], F32, name="x_bank")
-            x_got = after(("xg", b), ("nz", b - 1, 0), [P, 2, PASSES * P, 2], BF16)
-            nc.scalar.activation(
-                x_got[:].rearrange("q u p e -> q p u e"), x_win[b][:].indirect(offsets[:]), ACT.Copy
-            )
-            pairs = x_got[:].rearrange("q u p e -> q (u p e)").bitcast(F32)
+            x_banks[b] = psum.tile([P, PASSES, 2, P], F32, name="x_bank")
+            x_got = successor(("x_got", b), ("h_win", b) if b > 0 else None, [P, 2, PASSES * P, 2], BF16)
+            nc.scalar.activation(x_got[:].rearrange("d u r e -> d r u e"), x_win[b][:].indirect(offsets[:]), ACT.Copy)
+            pairs = x_got[:].rearrange("d u r e -> d (u r e)").bitcast(F32)
             for g in range(PASSES):
                 for u in range(2):
                     first = (u * PASSES + g) * P
-                    nc.tensor.transpose(bank[:, g, u, :], pairs[:, first : first + P], ident[:])
-            x_banks[b] = bank
+                    nc.tensor.transpose(x_banks[b][:, g, u, :], pairs[:, first : first + P], ident[:])
 
         def fetch_x(b):
-            turned = work.tile([P, PASSES * PASS], BF16, name="x_turned", align_bytes=64)
-            nc.scalar.copy(
-                turned[:].bitcast(F32).rearrange("p (g d u) -> p g d u", g=PASSES, u=2),
+            x_turned[b] = per_block.tile([P, PASSES * PASS], BF16, name="x_turned", align_bytes=MX_ALIGN)
+            move = nc.vector.tensor_copy if b == LAST else nc.scalar.copy
+            move(
+                x_turned[b][:].bitcast(F32).rearrange("p (g d u) -> p g d u", g=PASSES, u=2),
                 x_banks[b][:].rearrange("p g u d -> p g d u"),
             )
-            x_turned[b] = turned
 
         def quantize_x(b):
-            if b < 2:
-                pair = after(("xc", b), ("sq", BLOCKS - 1, b), [P, 2, PASSES * P], U32)
-                x_codes[b], x_codes[b + 2] = pair[:, 0, :], pair[:, 1, :]
-            nc.vector.quantize_mx(out=x_codes[b][:, :].bitcast(E4M3), scales=x_scales[b][:, :], in_=x_turned[b][:])
+            if b < PASSES:
+                both = successor(("x_codes", b), ("squares", LAST, b), [P, 2, PASSES * P], U32)
+                x_codes[b], x_codes[b + PASSES] = both[:, 0, :], both[:, 1, :]
+            nc.vector.quantize_mx(out=x_codes[b].bitcast(E4M3), scales=x_scales[b][:], in_=x_turned[b][:])
 
-        accs = [psum.tile([P, DV], F32, name="acc", bufs=4) for b in range(BLOCKS)]
+        accs = [psum.tile([P, DV], F32, name="acc", bufs=BLOCKS) for b in range(BLOCKS)]
 
         def multiply(b, g):
             cols = slice(g * P, (g + 1) * P)
@@ -195,46 +188,47 @@ def tile_attend_gex_tnh_w_kernel(tc, xT, dyT, hT, ts, offs, out):
                 out=accs[b][:],
                 lhsT=x_codes[b][:, cols].bitcast(E4M3),
                 lhsT_scale=x_scales[b][:, cols],
-                rhs=dz_codes[g][:, :].bitcast(E5M2),
-                rhs_scale=dz_scales[g][:, :],
+                rhs=dz_codes[g][:].bitcast(E5M2),
+                rhs_scale=dz_scales[g][:],
                 start=(g == 0),
                 stop=(g == PASSES - 1),
             )
 
         def store(b):
-            result = work.tile([P, DV], F32, name="result")
+            result = per_block.tile([P, DV], F32, name="result")
             if b % 2 == 0:
                 nc.scalar.activation(result[:], accs[b][:], ACT.Copy, scale=-1.0)
             else:
                 nc.vector.tensor_scalar_mul(result[:], accs[b][:], -1.0)
             nc.sync.dma_start(out[0, b * P : (b + 1) * P, :], result[:])
 
-        last = BLOCKS - 1
         for b in range(BLOCKS):
             gather_h(b)
             if b == 0:
-                gather_ts()
-            else:
-                fetch_dz(b - 1)
+                nc.vector.tensor_copy(ts_got[:], ts_win[:].indirect(offsets[:]))
+            square_h(b, 0)
             cast_x(b, 0)
-            cast_x(b, 1)
             if b > 0:
                 fetch_x(b - 1)
-            square_h(b, 0)
-            gather_x(b)
+            cast_x(b, 1)
+            if b > 0:
+                fetch_dz(b - 1)
             square_h(b, 1)
+            gather_x(b)
             for g in range(PASSES):
                 gather_dy(b, g)
             for g in range(PASSES):
                 form_dz(b, g)
-        fetch_x(last)
-        for b in range(BLOCKS):
+
+        for b in range(LAST):
             quantize_x(b)
-        fetch_dz(last)
+        fetch_dz(LAST)
         for g in range(PASSES):
-            dz_codes[g] = after(("dzc", g), ("dy", last, g), [P, DV], U32)
+            dz_codes[g] = successor(("dz_codes", g), ("dy_ts", LAST, g), [P, DV], U32)
             for b in range(BLOCKS):
                 quantize_dz(b, g)
+        fetch_x(LAST)
+        quantize_x(LAST)
         for b in range(BLOCKS):
             for g in range(PASSES):
                 multiply(b, g)

@@ -27,11 +27,10 @@ LIST_COLS = PASS // 16
 MX_ALIGN = 64
 
 TS_RUN = TOKENS // P
-TS_HALF = TS_RUN // 2
 BANK_COLS = 4
 
-LOAD_ORDER = [("h", 0), ("x", 0), ("dy", 0)] + [(kind, b) for b in range(1, BLOCKS) for kind in ("x", "h", "dy")]
-CASTS_ON_VECTOR = ((2, 0), (3, 1))
+KIB = 1024
+V_CAST = 512
 
 FLOPS = 2 * D * DV * SLOTS
 
@@ -40,154 +39,149 @@ def tile_attend_gex_tnh_w_kernel(tc, xT, dyT, hT, ts, offs, out):
     nc = tc.nc
     with ExitStack() as ctx:
         keep = ctx.enter_context(tc.tile_pool(name="keep", bufs=1))
-        per_block = ctx.enter_context(tc.tile_pool(name="per_block", bufs=BLOCKS))
+        placed = ctx.enter_context(tc.tile_pool(name="placed", bufs=1))
         psum = ctx.enter_context(tc.psum_pool(name="psum", bufs=1))
 
-        tag_of = {}
+        def own(name, shape, dtype):
+            return keep.tile(shape, dtype, name=name, align_bytes=MX_ALIGN)
 
-        def successor(key, previous, shape, dtype):
-            tag_of[key] = tag_of.get(previous, "-".join(map(str, key)))
-            return keep.tile(shape, dtype, name=tag_of[key], align_bytes=MX_ALIGN)
+        def place(name, shape, dtype, region, kib):
+            return placed.tile(shape, dtype, name=name, align_bytes=MX_ALIGN, offset=(8 * region + kib) * KIB)
 
         offsets = keep.tile([P, SLOTS // 16], U16, name="offsets")
-        ts_runs = ts[0, :].rearrange("(p j) -> p j", p=P)
-        ts_cols = [successor(("ts_cols", i), None, [P, TS_HALF], F32) for i in range(2)]
-        for i in range(2):
-            nc.sync.dma_start(ts_cols[i][:], ts_runs[:, TS_HALF * i : TS_HALF * (i + 1)])
+        ts_cols = place("ts_cols", [P, TS_RUN], F32, 0, 2)
+        nc.sync.dma_start(ts_cols[:], ts[0, :].rearrange("(p j) -> p j", p=P))
         pass_lists = [offsets[:, g * LIST_COLS : (g + 1) * LIST_COLS] for g in range(PASSES)]
         pass_slots = [slice(g * PASS, (g + 1) * PASS) for g in range(PASSES)]
+
+        def piece(b, k):
+            cut = TOKENS - V_CAST if 0 < b < LAST else TOKENS // 2
+            return slice(0, cut) if k == 0 else slice(cut, TOKENS)
 
         ident = keep.tile([P, P], F32, name="ident")
         make_identity(nc, ident[:])
 
-        h_win = [successor(("h_win", b), None, [P, TOKENS], F32) for b in range(BLOCKS)]
-        dy_win = [keep.tile([P, TOKENS], F32, name="dy_win%d" % b) for b in range(BLOCKS)]
-        x_raw = [keep.tile([P, TOKENS], F32, name="x_raw%d" % b) for b in range(BLOCKS)]
-        token_halves = [slice(0, TOKENS // 2), slice(TOKENS // 2, TOKENS)]
+        h_win = [own("h_win%d" % b, [P, TOKENS], F32) for b in range(BLOCKS)]
+        dy_win = [place("dy_win%d" % b, [P, TOKENS], F32, b + 2, 0) for b in range(BLOCKS)]
+        x_raw = {}
+        for b in range(BLOCKS):
+            for k in range(2):
+                x_raw[b, k] = own("x_raw%d_%d" % (b, k), [P, piece(b, k).stop - piece(b, k).start], F32)
 
-        for kind, b in LOAD_ORDER:
-            rows = slice(b * P, (b + 1) * P)
-            if kind == "h":
-                nc.sync.dma_start(h_win[b][:], hT[rows, :])
-            elif kind == "dy":
-                nc.sync.dma_start(dy_win[b][:], dyT[rows, :])
-            else:
-                for cols in token_halves:
-                    nc.sync.dma_start(x_raw[b][:, cols], xT[rows, cols])
-            if (kind, b) == LOAD_ORDER[0]:
+        def rows(b):
+            return slice(b * P, (b + 1) * P)
+
+        def load_x(b, k):
+            nc.sync.dma_start(x_raw[b, k][:], xT[rows(b), piece(b, k)])
+
+        def load_h(b):
+            nc.sync.dma_start(h_win[b][:], hT[rows(b), :])
+
+        def load_dy(b):
+            nc.sync.dma_start(dy_win[b][:], dyT[rows(b), :])
+
+        for b in range(LAST):
+            load_h(b)
+            if b == 0:
                 nc.sync.dma_start(offsets[:], offs)
+            load_x(b, 0)
+            load_x(b, 1)
+            load_dy(b)
+        load_h(LAST)
+        load_x(LAST, 0)
+        load_dy(LAST)
+        load_x(LAST, 1)
 
         ts_win = keep.tile([P, TOKENS], F32, name="ts_win")
         ts_view = ts_win[:].rearrange("m (p j) -> m p j", p=P)
-        for c in (0, 2, 1, 3):
+        for c in range(TS_RUN // BANK_COLS):
             spread = psum.tile([P, BANK_COLS, P], F32, name="acc", bufs=BLOCKS)
             for j in range(BANK_COLS):
-                col = BANK_COLS * (c % 2) + j
-                nc.tensor.transpose(spread[:, j, :], ts_cols[c // 2][:, col : col + 1].to_broadcast([P, P]), ident[:])
+                col = BANK_COLS * c + j
+                nc.tensor.transpose(spread[:, j, :], ts_cols[:, col : col + 1].to_broadcast([P, P]), ident[:])
             nc.scalar.copy(ts_view[:, :, BANK_COLS * c : BANK_COLS * (c + 1)], spread[:].rearrange("m j p -> m p j"))
 
-        ts_got = keep.tile([P, SLOTS], F32, name="ts_got")
-        dz_scales = [keep.tile([P, DV], U8, name="dz_scales%d" % g, align_bytes=MX_ALIGN) for g in range(PASSES)]
-        x_scales = [keep.tile([P, PASSES * P], U8, name="x_scales%d" % b, align_bytes=MX_ALIGN) for b in range(BLOCKS)]
+        ts_got = own("ts_got", [P, SLOTS], F32)
+        dz_scales = [own("dz_scales%d" % g, [P, DV], U8) for g in range(PASSES)]
         h_got, squares, dy_ts, dz_banks, dz_turned, dz_codes = {}, {}, {}, {}, {}, {}
-        x_win, x_banks, x_turned, x_codes = {}, {}, {}, {}
+        x_win, x_banks, x_codes, x_scales = {}, {}, {}, {}
 
         def gather_h(b):
-            h_got[b, 0] = successor(("h_got", b, 0), ("dy_ts", b - 1, 0), [P, PASS], F32)
-            h_got[b, 1] = successor(("h_got", b, 1), ("squares", b - 1, 0), [P, PASS], F32)
-            for g in range(PASSES):
-                nc.vector.tensor_copy(h_got[b, g][:], h_win[b][:].indirect(pass_lists[g]))
+            h_got[b] = place("h_got%d" % b, [P, SLOTS], F32, b + 1, 0)
+            nc.vector.tensor_copy(h_got[b][:], h_win[b][:].indirect(offsets[:]))
 
-        def square_h(b, g):
-            if b > 0:
-                squares[b, g] = successor(("squares", b, g), None, [P, PASS], F32)[:]
-            elif g == 0:
-                both = successor(("squares", 0, 0), ("ts_cols", 0), [P, SLOTS], F32)
-                squares[0, 0], squares[0, 1] = both[:, pass_slots[0]], both[:, pass_slots[1]]
-            nc.scalar.activation(squares[b, g], h_got[b, g][:], ACT.Square)
+        def square_h(b, tile):
+            squares[b] = tile
+            nc.scalar.activation(tile[:], h_got[b][:], ACT.Square)
 
-        def gather_dy(b, g):
-            if g == 0:
-                previous = ("dy_ts", b - 1, 1)
-            else:
-                previous = ("neg_dz", 0, 1) if b == 1 else ("squares", b - 1, 1)
-            dy_ts[b, g] = successor(("dy_ts", b, g), previous, [P, PASS], F32)
-            nc.vector.tensor_tensor(
-                dy_ts[b, g][:], dy_win[b][:].indirect(pass_lists[g]), ts_got[:, pass_slots[g]], ALU.mult
+        def gather_dy(b, listed, slots, tile):
+            nc.vector.tensor_tensor(tile[:], dy_win[b][:].indirect(listed), ts_got[:, slots], ALU.mult)
+            return tile
+
+        def form_dz(b, passes, scaled, neg_dz):
+            n = len(passes)
+            slots = slice(passes[0] * PASS, (passes[-1] + 1) * PASS)
+            nc.vector.scalar_tensor_tensor(neg_dz[:], squares[b][:, slots], 1.0, scaled[:], ALU.subtract, ALU.mult)
+            pairs = neg_dz[:].bitcast(F32).rearrange("n (g p u) -> n g u p", g=n, u=2)
+            bank = psum.tile([P, PASSES, 2, P], F32, name="dz_bank", bufs=2)
+            dz_banks[b, passes[0]] = bank
+            for i in range(n):
+                for u in range(2):
+                    nc.tensor.transpose(bank[:, i, u, :], pairs[:, i, u, :], ident[:])
+
+        def fetch_dz(b, passes, tile, move):
+            n = len(passes)
+            move(
+                tile[:].bitcast(F32).rearrange("p (g n u) -> p g n u", g=n, u=2),
+                dz_banks[b, passes[0]][:, 0:n].rearrange("p g u n -> p g n u"),
             )
-
-        def form_dz(b, g):
-            neg_dz = successor(("neg_dz", b, g), None, [P, PASS], BF16)
-            nc.vector.scalar_tensor_tensor(neg_dz[:], squares[b, g], 1.0, dy_ts[b, g][:], ALU.subtract, ALU.mult)
-            pairs = neg_dz[:].bitcast(F32).rearrange("n (p u) -> n u p", u=2)
-            if b == LAST:
-                if g == 0:
-                    dz_banks[b, g] = psum.tile([P, 2, P], F32, name="dz_bank", bufs=2)[:]
-                else:
-                    dz_banks[b, g] = psum.tile([P, 2, P], F32, name="dz_bank_last")[:]
-            elif g == 0:
-                dz_banks[b] = psum.tile([P, PASSES, 2, P], F32, name="dz_bank", bufs=2)
-                dz_banks[b, 0], dz_banks[b, 1] = dz_banks[b][:, 0], dz_banks[b][:, 1]
-            for u in range(2):
-                nc.tensor.transpose(dz_banks[b, g][:, u, :], pairs[:, u, :], ident[:])
-
-        def fetch_dz(b):
-            dz_turned[b] = per_block.tile([P, PASSES, PASS], BF16, name="dz_turned", align_bytes=MX_ALIGN)
-            pairs = dz_turned[b][:].rearrange("p g k -> p (g k)").bitcast(F32)
-            pairs = pairs.rearrange("p (g n u) -> p g n u", g=PASSES, u=2)
-            if b < LAST:
-                nc.scalar.copy(pairs, dz_banks[b][:].rearrange("p g u n -> p g n u"))
-            else:
-                for g in range(PASSES):
-                    nc.scalar.copy(pairs[:, g], dz_banks[b, g].rearrange("p u n -> p n u"))
+            for i in range(n):
+                dz_turned[b, passes[i]] = tile[:, pass_slots[i]]
 
         def quantize_dz(b, g):
-            cols = slice(b * P, (b + 1) * P)
-            nc.vector.quantize_mx(
-                out=dz_codes[g][:, cols].bitcast(E5M2), scales=dz_scales[g][:, cols], in_=dz_turned[b][:, g, :]
-            )
+            codes = dz_codes[g][:, rows(b)].bitcast(E5M2)
+            nc.vector.quantize_mx(out=codes, scales=dz_scales[g][:, rows(b)], in_=dz_turned[b, g])
 
-        def cast_x(b, half):
-            if half == 0:
-                x_win[b] = successor(("x_win", b), ("ts_cols", 1) if b == 0 else None, [P, TOKENS], BF16)
-            cols = token_halves[half]
-            if (b, half) in CASTS_ON_VECTOR:
-                nc.vector.tensor_copy(x_win[b][:, cols], x_raw[b][:, cols])
+        def cast_x(b, k):
+            if k == 0:
+                x_win[b] = place("x_win%d" % b, [P, TOKENS], BF16, b, 2)
+            if k == 1 and 0 < b < LAST:
+                nc.vector.tensor_copy(x_win[b][:, piece(b, k)], x_raw[b, k][:])
             else:
-                nc.scalar.activation(x_win[b][:, cols], x_raw[b][:, cols], ACT.Copy)
+                nc.scalar.activation(x_win[b][:, piece(b, k)], x_raw[b, k][:], ACT.Copy)
 
-        def gather_x(b):
-            x_banks[b] = psum.tile([P, PASSES, 2, P], F32, name="x_bank")
-            x_got = successor(("x_got", b), ("h_win", b) if b > 0 else None, [P, 2, PASSES * P, 2], BF16)
-            nc.scalar.activation(x_got[:].rearrange("d u r e -> d r u e"), x_win[b][:].indirect(offsets[:]), ACT.Copy)
+        def gather_x(b, passes, listed, x_got):
+            n = len(passes)
+            nc.scalar.activation(x_got[:].rearrange("d u r e -> d r u e"), x_win[b][:].indirect(listed), ACT.Copy)
             pairs = x_got[:].rearrange("d u r e -> d (u r e)").bitcast(F32)
-            for g in range(PASSES):
+            bank = psum.tile([P, PASSES, 2, P], F32, name="x_bank", bufs=2)
+            x_banks[b] = bank
+            for i in range(n):
+                x_banks[b, passes[i]] = bank[:, i]
                 for u in range(2):
-                    first = (u * PASSES + g) * P
-                    nc.tensor.transpose(x_banks[b][:, g, u, :], pairs[:, first : first + P], ident[:])
+                    first = (u * n + i) * P
+                    nc.tensor.transpose(bank[:, i, u, :], pairs[:, first : first + P], ident[:])
+
+        x_turned = [own("x_turned%d" % b, [P, SLOTS], BF16) for b in range(BLOCKS)]
 
         def fetch_x(b):
-            x_turned[b] = per_block.tile([P, PASSES * PASS], BF16, name="x_turned", align_bytes=MX_ALIGN)
-            move = nc.vector.tensor_copy if b == LAST else nc.scalar.copy
-            move(
+            nc.scalar.copy(
                 x_turned[b][:].bitcast(F32).rearrange("p (g d u) -> p g d u", g=PASSES, u=2),
                 x_banks[b][:].rearrange("p g u d -> p g d u"),
             )
 
-        def quantize_x(b):
-            if b < PASSES:
-                both = successor(("x_codes", b), ("squares", LAST, b), [P, 2, PASSES * P], U32)
-                x_codes[b], x_codes[b + PASSES] = both[:, 0, :], both[:, 1, :]
-            nc.vector.quantize_mx(out=x_codes[b].bitcast(E4M3), scales=x_scales[b][:], in_=x_turned[b][:])
+        def quantize_x(b, codes):
+            x_codes[b] = codes
+            x_scales[b] = own("x_scales%d" % b, [P, PASSES * P], U8)
+            nc.vector.quantize_mx(out=x_codes[b][:].bitcast(E4M3), scales=x_scales[b][:], in_=x_turned[b][:])
 
         accs = [psum.tile([P, DV], F32, name="acc", bufs=BLOCKS) for b in range(BLOCKS)]
 
         def multiply(b, g):
-            cols = slice(g * P, (g + 1) * P)
             nc.tensor.matmul_mx(
                 out=accs[b][:],
-                lhsT=x_codes[b][:, cols].bitcast(E4M3),
-                lhsT_scale=x_scales[b][:, cols],
+                lhsT=x_codes[b][:, rows(g)].bitcast(E4M3),
+                lhsT_scale=x_scales[b][:, rows(g)],
                 rhs=dz_codes[g][:].bitcast(E5M2),
                 rhs_scale=dz_scales[g][:],
                 start=(g == 0),
@@ -195,41 +189,57 @@ def tile_attend_gex_tnh_w_kernel(tc, xT, dyT, hT, ts, offs, out):
             )
 
         def store(b):
-            result = per_block.tile([P, DV], F32, name="result")
+            result = own("result%d" % b, [P, DV], F32)
             if b % 2 == 0:
                 nc.scalar.activation(result[:], accs[b][:], ACT.Copy, scale=-1.0)
             else:
                 nc.vector.tensor_scalar_mul(result[:], accs[b][:], -1.0)
-            nc.sync.dma_start(out[0, b * P : (b + 1) * P, :], result[:])
+            nc.sync.dma_start(out[0, rows(b), :], result[:])
 
-        for b in range(BLOCKS):
-            gather_h(b)
-            if b == 0:
-                nc.vector.tensor_copy(ts_got[:], ts_win[:].indirect(offsets[:]))
-            square_h(b, 0)
-            cast_x(b, 0)
-            if b > 0:
-                fetch_x(b - 1)
-            cast_x(b, 1)
-            if b > 0:
-                fetch_dz(b - 1)
-            square_h(b, 1)
-            gather_x(b)
-            for g in range(PASSES):
-                gather_dy(b, g)
-            for g in range(PASSES):
-                form_dz(b, g)
-
-        for b in range(LAST):
-            quantize_x(b)
-        fetch_dz(LAST)
+        both = (0, 1)
+        gather_h(0)
         for g in range(PASSES):
-            dz_codes[g] = successor(("dz_codes", g), ("dy_ts", LAST, g), [P, DV], U32)
-            for b in range(BLOCKS):
-                quantize_dz(b, g)
+            nc.vector.tensor_copy(ts_got[:, pass_slots[g]], ts_win[:].indirect(pass_lists[g]))
+        cast_x(0, 0)
+        cast_x(0, 1)
+        for b in range(LAST):
+            gather_x(b, both, offsets[:], own("x_got%d" % b, [P, 2, PASSES * P, 2], BF16))
+            if b > 0:
+                fetch_dz(b - 1, both, place("dz_turned%d" % (b - 1), [P, SLOTS], BF16, b, 4), nc.scalar.copy)
+            square_h(b, place("squares%d" % b, [P, SLOTS], F32, b, 0))
+            fetch_x(b)
+            scaled = gather_dy(b, offsets[:], slice(0, SLOTS), place("dy_ts%d" % b, [P, SLOTS], F32, BLOCKS + 3, 2))
+            gather_h(b + 1)
+            cast_x(b + 1, 0)
+            if b + 1 < LAST:
+                cast_x(b + 1, 1)
+            form_dz(b, both, scaled, own("neg_dz%d" % b, [P, SLOTS], BF16))
+            quantize_x(b, own("x_codes%d" % b, [P, PASSES * P], U32))
+
+        tail = BLOCKS + 2
+        square_h(LAST, place("squares3", [P, SLOTS], F32, LAST - 1, 6))
+        cast_x(LAST, 1)
+        fetch_dz(LAST - 1, both, own("dz_turned2", [P, SLOTS], BF16), nc.scalar.copy)
+        scaled = gather_dy(LAST, pass_lists[0], pass_slots[0], place("dy_ts3_0", [P, PASS], F32, tail + 1, 1))
+        form_dz(LAST, (0,), scaled, own("neg_dz3_0", [P, PASS], BF16))
+        dz_codes[0] = place("dz_codes0", [P, DV], U32, tail + 1, 0)
+        for b in range(LAST):
+            quantize_dz(b, 0)
+        fetch_dz(LAST, (0,), place("dz_turned3_0", [P, PASS], BF16, tail, 1), nc.vector.tensor_copy)
+        quantize_dz(LAST, 0)
+        for b in range(LAST):
+            multiply(b, 0)
+        gather_x(LAST, both, offsets[:], own("x_got3", [P, 2, PASSES * P, 2], BF16))
+        scaled = gather_dy(LAST, pass_lists[1], pass_slots[1], place("dy_ts3_1", [P, PASS], F32, tail, 1))
+        dz_codes[1] = own("ts_got", [P, DV], U32)
+        for b in range(LAST):
+            quantize_dz(b, 1)
+        form_dz(LAST, (1,), scaled, own("neg_dz3_1", [P, PASS], BF16))
         fetch_x(LAST)
-        quantize_x(LAST)
+        quantize_x(LAST, place("x_codes3", [P, PASSES * P], U32, tail, 2))
+        fetch_dz(LAST, (1,), own("dz_turned3_1", [P, PASS], BF16), nc.scalar.copy)
+        quantize_dz(LAST, 1)
+        multiply(LAST, 0)
         for b in range(BLOCKS):
-            for g in range(PASSES):
-                multiply(b, g)
+            multiply(b, 1)
             store(b)

@@ -152,15 +152,14 @@ def tile_attend_gex_tnh_w_kernel(tc, xT, dyT, hT, ts, offs, out):
 
         def gather_x(b, passes, listed, x_got):
             n = len(passes)
-            nc.scalar.activation(x_got[:].rearrange("d u r e -> d r u e"), x_win[b][:].indirect(listed), ACT.Copy)
-            pairs = x_got[:].rearrange("d u r e -> d (u r e)").bitcast(F32)
+            nc.scalar.activation(x_got[:], x_win[b][:].indirect(listed), ACT.Copy)
+            pairs = x_got[:].bitcast(F32).rearrange("d (g p u) -> d g u p", g=n, u=2)
             bank = psum.tile([P, PASSES, 2, P], F32, name="x_bank", bufs=2)
             x_banks[b] = bank
             for i in range(n):
                 x_banks[b, passes[i]] = bank[:, i]
                 for u in range(2):
-                    first = (u * n + i) * P
-                    nc.tensor.transpose(bank[:, i, u, :], pairs[:, first : first + P], ident[:])
+                    nc.tensor.transpose(bank[:, i, u, :], pairs[:, i, u, :], ident[:])
 
         x_turned = [own("x_turned%d" % b, [P, SLOTS], BF16) for b in range(BLOCKS)]
 
@@ -203,7 +202,7 @@ def tile_attend_gex_tnh_w_kernel(tc, xT, dyT, hT, ts, offs, out):
         cast_x(0, 0)
         cast_x(0, 1)
         for b in range(LAST):
-            gather_x(b, both, offsets[:], own("x_got%d" % b, [P, 2, PASSES * P, 2], BF16))
+            gather_x(b, both, offsets[:], own("x_got%d" % b, [P, SLOTS], BF16))
             if b > 0:
                 fetch_dz(b - 1, both, place("dz_turned%d" % (b - 1), [P, SLOTS], BF16, b, 4), nc.scalar.copy)
             square_h(b, place("squares%d" % b, [P, SLOTS], F32, b, 0))
@@ -229,17 +228,19 @@ def tile_attend_gex_tnh_w_kernel(tc, xT, dyT, hT, ts, offs, out):
         quantize_dz(LAST, 0)
         for b in range(LAST):
             multiply(b, 0)
-        gather_x(LAST, both, offsets[:], own("x_got3", [P, 2, PASSES * P, 2], BF16))
+        gather_x(LAST, both, offsets[:], own("x_got3", [P, SLOTS], BF16))
         scaled = gather_dy(LAST, pass_lists[1], pass_slots[1], place("dy_ts3_1", [P, PASS], F32, tail, 1))
         dz_codes[1] = own("ts_got", [P, DV], U32)
         for b in range(LAST):
             quantize_dz(b, 1)
         form_dz(LAST, (1,), scaled, own("neg_dz3_1", [P, PASS], BF16))
         fetch_x(LAST)
-        quantize_x(LAST, place("x_codes3", [P, PASSES * P], U32, tail, 2))
-        fetch_dz(LAST, (1,), own("dz_turned3_1", [P, PASS], BF16), nc.scalar.copy)
+        fetch_dz(LAST, (1,), place("dz_turned3_1", [P, PASS], BF16, tail, 1), nc.vector.tensor_copy)
         quantize_dz(LAST, 1)
-        multiply(LAST, 0)
-        for b in range(BLOCKS):
+        quantize_x(LAST, place("x_codes3", [P, PASSES * P], U32, tail, 1))
+        for b in range(LAST):
             multiply(b, 1)
             store(b)
+        multiply(LAST, 0)
+        multiply(LAST, 1)
+        store(LAST)

@@ -30,7 +30,9 @@ TS_RUN = TOKENS // P
 BANK_COLS = 4
 
 KIB = 1024
-V_CAST = 512
+LANE_KIB = 8
+X_LANE = BLOCKS + 1
+TAIL_LANE = X_LANE + BLOCKS
 
 FLOPS = 2 * D * DV * SLOTS
 
@@ -45,54 +47,39 @@ def tile_attend_gex_tnh_w_kernel(tc, xT, dyT, hT, ts, offs, out):
         def own(name, shape, dtype):
             return keep.tile(shape, dtype, name=name, align_bytes=MX_ALIGN)
 
-        def place(name, shape, dtype, region, kib):
-            return placed.tile(shape, dtype, name=name, align_bytes=MX_ALIGN, offset=(8 * region + kib) * KIB)
+        def place(name, shape, dtype, lane, kib):
+            offset = int((LANE_KIB * lane + kib) * KIB)
+            return placed.tile(shape, dtype, name=name, align_bytes=MX_ALIGN, offset=offset)
+
+        def rows(b):
+            return slice(b * P, (b + 1) * P)
 
         offsets = keep.tile([P, SLOTS // 16], U16, name="offsets")
-        ts_cols = place("ts_cols", [P, TS_RUN], F32, 0, 2)
+        ts_cols = place("ts_cols", [P, TS_RUN], F32, X_LANE, 5)
         nc.sync.dma_start(ts_cols[:], ts[0, :].rearrange("(p j) -> p j", p=P))
         pass_lists = [offsets[:, g * LIST_COLS : (g + 1) * LIST_COLS] for g in range(PASSES)]
         pass_slots = [slice(g * PASS, (g + 1) * PASS) for g in range(PASSES)]
-
-        def piece(b, k):
-            cut = TOKENS - V_CAST if 0 < b < LAST else TOKENS // 2
-            return slice(0, cut) if k == 0 else slice(cut, TOKENS)
+        token_halves = [slice(0, TOKENS // 2), slice(TOKENS // 2, TOKENS)]
 
         ident = keep.tile([P, P], F32, name="ident")
         make_identity(nc, ident[:])
 
         h_win = [own("h_win%d" % b, [P, TOKENS], F32) for b in range(BLOCKS)]
-        dy_win = [place("dy_win%d" % b, [P, TOKENS], F32, b + 2, 0) for b in range(BLOCKS)]
+        dy_win = [own("dy_win%d" % b, [P, TOKENS], F32) for b in range(BLOCKS)]
         x_raw = {}
         for b in range(BLOCKS):
-            for k in range(2):
-                x_raw[b, k] = own("x_raw%d_%d" % (b, k), [P, piece(b, k).stop - piece(b, k).start], F32)
+            x_raw[b, 0] = own("x_raw%d_0" % b, [P, TOKENS // 2], F32)
+            x_raw[b, 1] = place("x_raw%d_1" % b, [P, TOKENS // 2], F32, b + 1, 4)
 
-        def rows(b):
-            return slice(b * P, (b + 1) * P)
-
-        def load_x(b, k):
-            nc.sync.dma_start(x_raw[b, k][:], xT[rows(b), piece(b, k)])
-
-        def load_h(b):
+        for b in range(BLOCKS):
             nc.sync.dma_start(h_win[b][:], hT[rows(b), :])
-
-        def load_dy(b):
-            nc.sync.dma_start(dy_win[b][:], dyT[rows(b), :])
-
-        for b in range(LAST):
-            load_h(b)
             if b == 0:
                 nc.sync.dma_start(offsets[:], offs)
-            load_x(b, 0)
-            load_x(b, 1)
-            load_dy(b)
-        load_h(LAST)
-        load_x(LAST, 0)
-        load_dy(LAST)
-        load_x(LAST, 1)
+            for half in range(2):
+                nc.sync.dma_start(x_raw[b, half][:], xT[rows(b), token_halves[half]])
+            nc.sync.dma_start(dy_win[b][:], dyT[rows(b), :])
 
-        ts_win = keep.tile([P, TOKENS], F32, name="ts_win")
+        ts_win = own("ts_win", [P, TOKENS], F32)
         ts_view = ts_win[:].rearrange("m (p j) -> m p j", p=P)
         for c in range(TS_RUN // BANK_COLS):
             spread = psum.tile([P, BANK_COLS, P], F32, name="acc", bufs=BLOCKS)
@@ -103,76 +90,55 @@ def tile_attend_gex_tnh_w_kernel(tc, xT, dyT, hT, ts, offs, out):
 
         ts_got = own("ts_got", [P, SLOTS], F32)
         dz_scales = [own("dz_scales%d" % g, [P, DV], U8) for g in range(PASSES)]
-        h_got, squares, dy_ts, dz_banks, dz_turned, dz_codes = {}, {}, {}, {}, {}, {}
-        x_win, x_banks, x_codes, x_scales = {}, {}, {}, {}
+        dz_banks, dz_turned, dz_codes = {}, {}, {}
+        x_banks, x_turned, x_codes, x_scales = {}, {}, {}, {}
 
-        def gather_h(b):
-            h_got[b] = place("h_got%d" % b, [P, SLOTS], F32, b + 1, 0)
-            nc.vector.tensor_copy(h_got[b][:], h_win[b][:].indirect(offsets[:]))
+        def form_dz(b, g, squares, dy_ts):
+            if (b, g) == (LAST, PASSES - 1):
+                neg_dz = place("neg_dz_last", [P, PASS], BF16, TAIL_LANE, 1.5)
+            else:
+                neg_dz = own("neg_dz%d_%d" % (b, g), [P, PASS], BF16)
+            nc.vector.scalar_tensor_tensor(neg_dz[:], squares[:, pass_slots[g]], 1.0, dy_ts[:], ALU.subtract, ALU.mult)
+            pairs = neg_dz[:].bitcast(F32).rearrange("n (p u) -> n u p", u=2)
+            if g == 0 or b == LAST:
+                dz_banks[b, g] = psum.tile([P, PASSES, 2, P], F32, name="dz_bank", bufs=2)
+            bank = dz_banks[b, g][:, 0] if b == LAST else dz_banks[b, 0][:, g]
+            for u in range(2):
+                nc.tensor.transpose(bank[:, u, :], pairs[:, u, :], ident[:])
 
-        def square_h(b, tile):
-            squares[b] = tile
-            nc.scalar.activation(tile[:], h_got[b][:], ACT.Square)
-
-        def gather_dy(b, listed, slots, tile):
-            nc.vector.tensor_tensor(tile[:], dy_win[b][:].indirect(listed), ts_got[:, slots], ALU.mult)
-            return tile
-
-        def form_dz(b, passes, scaled, neg_dz):
+        def fetch_dz(b, passes, tile):
             n = len(passes)
-            slots = slice(passes[0] * PASS, (passes[-1] + 1) * PASS)
-            nc.vector.scalar_tensor_tensor(neg_dz[:], squares[b][:, slots], 1.0, scaled[:], ALU.subtract, ALU.mult)
-            pairs = neg_dz[:].bitcast(F32).rearrange("n (g p u) -> n g u p", g=n, u=2)
-            bank = psum.tile([P, PASSES, 2, P], F32, name="dz_bank", bufs=2)
-            dz_banks[b, passes[0]] = bank
-            for i in range(n):
-                for u in range(2):
-                    nc.tensor.transpose(bank[:, i, u, :], pairs[:, i, u, :], ident[:])
-
-        def fetch_dz(b, passes, tile, move):
-            n = len(passes)
-            move(
+            nc.scalar.copy(
                 tile[:].bitcast(F32).rearrange("p (g n u) -> p g n u", g=n, u=2),
                 dz_banks[b, passes[0]][:, 0:n].rearrange("p g u n -> p g n u"),
             )
-            for i in range(n):
-                dz_turned[b, passes[i]] = tile[:, pass_slots[i]]
+            for i, g in enumerate(passes):
+                dz_turned[b, g] = tile[:, pass_slots[i]]
 
         def quantize_dz(b, g):
             codes = dz_codes[g][:, rows(b)].bitcast(E5M2)
             nc.vector.quantize_mx(out=codes, scales=dz_scales[g][:, rows(b)], in_=dz_turned[b, g])
 
-        def cast_x(b, k):
-            if k == 0:
-                x_win[b] = place("x_win%d" % b, [P, TOKENS], BF16, b, 2)
-            if k == 1 and 0 < b < LAST:
-                nc.vector.tensor_copy(x_win[b][:, piece(b, k)], x_raw[b, k][:])
-            else:
-                nc.scalar.activation(x_win[b][:, piece(b, k)], x_raw[b, k][:], ACT.Copy)
-
-        def gather_x(b, passes, listed, x_got):
-            n = len(passes)
-            nc.scalar.activation(x_got[:], x_win[b][:].indirect(listed), ACT.Copy)
-            pairs = x_got[:].bitcast(F32).rearrange("d (g p u) -> d g u p", g=n, u=2)
-            bank = psum.tile([P, PASSES, 2, P], F32, name="x_bank", bufs=2)
-            x_banks[b] = bank
-            for i in range(n):
-                x_banks[b, passes[i]] = bank[:, i]
+        def gather_x(b, x_win, x_got):
+            laid = x_got[:].rearrange("d (u r e) -> d r u e", u=2, e=2)
+            nc.scalar.activation(laid, x_win[:].indirect(offsets[:]), ACT.Copy)
+            pairs = x_got[:].bitcast(F32).rearrange("d (u g p) -> d g u p", g=PASSES, u=2)
+            x_banks[b] = psum.tile([P, PASSES, 2, P], F32, name="x_bank", bufs=2)
+            for g in range(PASSES):
                 for u in range(2):
-                    nc.tensor.transpose(bank[:, i, u, :], pairs[:, i, u, :], ident[:])
+                    nc.tensor.transpose(x_banks[b][:, g, u, :], pairs[:, g, u, :], ident[:])
 
-        x_turned = [own("x_turned%d" % b, [P, SLOTS], BF16) for b in range(BLOCKS)]
-
-        def fetch_x(b):
+        def fetch_x(b, turned):
+            x_turned[b] = turned
             nc.scalar.copy(
-                x_turned[b][:].bitcast(F32).rearrange("p (g d u) -> p g d u", g=PASSES, u=2),
+                turned.bitcast(F32).rearrange("p (g d u) -> p g d u", g=PASSES, u=2),
                 x_banks[b][:].rearrange("p g u d -> p g d u"),
             )
 
         def quantize_x(b, codes):
             x_codes[b] = codes
             x_scales[b] = own("x_scales%d" % b, [P, PASSES * P], U8)
-            nc.vector.quantize_mx(out=x_codes[b][:].bitcast(E4M3), scales=x_scales[b][:], in_=x_turned[b][:])
+            nc.vector.quantize_mx(out=codes[:].bitcast(E4M3), scales=x_scales[b][:], in_=x_turned[b])
 
         accs = [psum.tile([P, DV], F32, name="acc", bufs=BLOCKS) for b in range(BLOCKS)]
 
@@ -189,58 +155,67 @@ def tile_attend_gex_tnh_w_kernel(tc, xT, dyT, hT, ts, offs, out):
 
         def store(b):
             result = own("result%d" % b, [P, DV], F32)
-            if b % 2 == 0:
+            if b % 2 == 1:
                 nc.scalar.activation(result[:], accs[b][:], ACT.Copy, scale=-1.0)
             else:
                 nc.vector.tensor_scalar_mul(result[:], accs[b][:], -1.0)
             nc.sync.dma_start(out[0, rows(b), :], result[:])
 
-        both = (0, 1)
-        gather_h(0)
-        for g in range(PASSES):
-            nc.vector.tensor_copy(ts_got[:, pass_slots[g]], ts_win[:].indirect(pass_lists[g]))
-        cast_x(0, 0)
-        cast_x(0, 1)
-        for b in range(LAST):
-            gather_x(b, both, offsets[:], own("x_got%d" % b, [P, SLOTS], BF16))
-            if b > 0:
-                fetch_dz(b - 1, both, place("dz_turned%d" % (b - 1), [P, SLOTS], BF16, b, 4), nc.scalar.copy)
-            square_h(b, place("squares%d" % b, [P, SLOTS], F32, b, 0))
-            fetch_x(b)
-            scaled = gather_dy(b, offsets[:], slice(0, SLOTS), place("dy_ts%d" % b, [P, SLOTS], F32, BLOCKS + 3, 2))
-            gather_h(b + 1)
-            cast_x(b + 1, 0)
-            if b + 1 < LAST:
-                cast_x(b + 1, 1)
-            form_dz(b, both, scaled, own("neg_dz%d" % b, [P, SLOTS], BF16))
+        all_passes = tuple(range(PASSES))
+        for b in range(BLOCKS):
+            x_win = place("x_win%d" % b, [P, TOKENS], BF16, X_LANE + b, 2)
+            for half in range(2):
+                nc.scalar.activation(x_win[:, token_halves[half]], x_raw[b, half][:], ACT.Copy)
+            if b == 2:
+                fetch_x(b - 1, own("x_raw%d_0" % b, [P, SLOTS], BF16)[:])
+
+            if b == 0:
+                h_got = own("h_got0", [P, SLOTS], F32)
+            else:
+                h_got = place("h_got%d" % b, [P, SLOTS], F32, b - 1, 1)
+            nc.vector.tensor_copy(h_got[:], h_win[b][:].indirect(offsets[:]))
+            if b == 0:
+                for g in range(PASSES):
+                    nc.vector.tensor_copy(ts_got[:, pass_slots[g]], ts_win[:].indirect(pass_lists[g]))
+            if b >= 2:
+                quantize_x(b - 2, place("x_codes%d" % (b - 2), [P, PASSES * P], U32, b - 1, 5))
+
+            if b < LAST:
+                x_got = place("x_got%d" % b, [P, SLOTS], BF16, X_LANE + b + 1, 5)
+            else:
+                x_got = own("x_got%d" % b, [P, SLOTS], BF16)
+            gather_x(b, x_win, x_got)
+            squares = place("squares%d" % b, [P, SLOTS], F32, b + 1, 4)
+            for g in range(PASSES):
+                nc.scalar.activation(squares[:, pass_slots[g]], h_got[:, pass_slots[g]], ACT.Square)
+            if b == 0:
+                fetch_x(b, own("x_turned0", [P, SLOTS], BF16)[:])
+            else:
+                fetch_dz(b - 1, all_passes, place("dz_turned%d" % (b - 1), [P, SLOTS], BF16, X_LANE + b, 2))
+
+            dy_ts = [place("dy_ts%d_%d" % (b, g), [P, PASS], F32, b, 4 + 2 * g) for g in range(PASSES)]
+            for g in range(PASSES):
+                gathered = dy_win[b][:].indirect(pass_lists[g])
+                nc.vector.tensor_tensor(dy_ts[g][:], gathered, ts_got[:, pass_slots[g]], ALU.mult)
+            for g in range(PASSES):
+                form_dz(b, g, squares, dy_ts[g])
+
+        for g, (lane, kib) in enumerate(((LAST, 3), (TAIL_LANE, 0))):
+            dz_codes[g] = place("dz_codes%d" % g, [P, DV], U32, lane, kib)
+            for b in range(LAST):
+                quantize_dz(b, g)
+            fetch_dz(LAST, (g,), own("dz_turned%d_%d" % (LAST, g), [P, PASS], BF16))
+            quantize_dz(LAST, g)
+
+        late = place("late_turned", [P, 2, SLOTS], BF16, TAIL_LANE, 2)
+        for i, b in enumerate((LAST - 1, LAST)):
+            fetch_x(b, late[:, i])
             quantize_x(b, own("x_codes%d" % b, [P, PASSES * P], U32))
 
-        tail = BLOCKS + 2
-        square_h(LAST, place("squares3", [P, SLOTS], F32, LAST - 1, 6))
-        cast_x(LAST, 1)
-        fetch_dz(LAST - 1, both, own("dz_turned2", [P, SLOTS], BF16), nc.scalar.copy)
-        scaled = gather_dy(LAST, pass_lists[0], pass_slots[0], place("dy_ts3_0", [P, PASS], F32, tail + 1, 1))
-        form_dz(LAST, (0,), scaled, own("neg_dz3_0", [P, PASS], BF16))
-        dz_codes[0] = place("dz_codes0", [P, DV], U32, tail + 1, 0)
-        for b in range(LAST):
-            quantize_dz(b, 0)
-        fetch_dz(LAST, (0,), place("dz_turned3_0", [P, PASS], BF16, tail, 1), nc.vector.tensor_copy)
-        quantize_dz(LAST, 0)
-        for b in range(LAST):
-            multiply(b, 0)
-        gather_x(LAST, both, offsets[:], own("x_got3", [P, SLOTS], BF16))
-        scaled = gather_dy(LAST, pass_lists[1], pass_slots[1], place("dy_ts3_1", [P, PASS], F32, tail, 1))
-        dz_codes[1] = own("ts_got", [P, DV], U32)
-        for b in range(LAST):
-            quantize_dz(b, 1)
-        form_dz(LAST, (1,), scaled, own("neg_dz3_1", [P, PASS], BF16))
-        fetch_x(LAST)
-        fetch_dz(LAST, (1,), place("dz_turned3_1", [P, PASS], BF16, tail, 1), nc.vector.tensor_copy)
-        quantize_dz(LAST, 1)
-        quantize_x(LAST, place("x_codes3", [P, PASSES * P], U32, tail, 1))
-        for b in range(LAST):
+        multiply(0, 0)
+        multiply(1, 0)
+        for b in range(BLOCKS):
+            if b > 1:
+                multiply(b, 0)
             multiply(b, 1)
             store(b)
-        multiply(LAST, 0)
-        multiply(LAST, 1)
-        store(LAST)

@@ -31,7 +31,7 @@ BANK_COLS = 4
 
 KIB = 1024
 LANE_KIB = 8
-X_LANE = BLOCKS + 1
+X_LANE = BLOCKS
 TAIL_LANE = X_LANE + BLOCKS
 
 FLOPS = 2 * D * DV * SLOTS
@@ -67,17 +67,29 @@ def tile_attend_gex_tnh_w_kernel(tc, xT, dyT, hT, ts, offs, out):
         h_win = [own("h_win%d" % b, [P, TOKENS], F32) for b in range(BLOCKS)]
         dy_win = [own("dy_win%d" % b, [P, TOKENS], F32) for b in range(BLOCKS)]
         x_raw = {}
-        for b in range(BLOCKS):
+        x_pieces = {}
+        for b in range(LAST):
+            x_pieces[b] = token_halves
             x_raw[b, 0] = own("x_raw%d_0" % b, [P, TOKENS // 2], F32)
             x_raw[b, 1] = place("x_raw%d_1" % b, [P, TOKENS // 2], F32, b + 1, 4)
+        x_pieces[LAST] = [slice(0, 1024), slice(1024, 1536), slice(1536, 2048)]
+        x_raw[LAST, 0] = place("x_raw_last0", [P, 1024], F32, TAIL_LANE, 4)
+        x_raw[LAST, 1] = own("x_raw_last1", [P, 512], F32)
+        x_raw[LAST, 2] = place("x_raw_last2", [P, 512], F32, TAIL_LANE, 14)
 
         for b in range(BLOCKS):
-            nc.sync.dma_start(h_win[b][:], hT[rows(b), :])
+            if b < LAST:
+                nc.sync.dma_start(h_win[b][:], hT[rows(b), :])
             if b == 0:
                 nc.sync.dma_start(offsets[:], offs)
-            for half in range(2):
-                nc.sync.dma_start(x_raw[b, half][:], xT[rows(b), token_halves[half]])
+            early = 2 if b < LAST else 1
+            for i, piece in enumerate(x_pieces[b][:early]):
+                nc.sync.dma_start(x_raw[b, i][:], xT[rows(b), piece])
+            if b == LAST - 1:
+                nc.sync.dma_start(h_win[LAST][:], hT[rows(LAST), :])
             nc.sync.dma_start(dy_win[b][:], dyT[rows(b), :])
+        for i in (1, 2):
+            nc.sync.dma_start(x_raw[LAST, i][:], xT[rows(LAST), x_pieces[LAST][i]])
 
         ts_win = own("ts_win", [P, TOKENS], F32)
         ts_view = ts_win[:].rearrange("m (p j) -> m p j", p=P)
@@ -88,29 +100,26 @@ def tile_attend_gex_tnh_w_kernel(tc, xT, dyT, hT, ts, offs, out):
                 nc.tensor.transpose(spread[:, j, :], ts_cols[:, col : col + 1].to_broadcast([P, P]), ident[:])
             nc.scalar.copy(ts_view[:, :, BANK_COLS * c : BANK_COLS * (c + 1)], spread[:].rearrange("m j p -> m p j"))
 
-        ts_got = own("ts_got", [P, SLOTS], F32)
+        ts_got = [place("ts_got0", [P, PASS], F32, TAIL_LANE, 18), place("ts_got1", [P, PASS], F32, TAIL_LANE, 22)]
         dz_scales = [own("dz_scales%d" % g, [P, DV], U8) for g in range(PASSES)]
         dz_banks, dz_turned, dz_codes = {}, {}, {}
         x_banks, x_turned, x_codes, x_scales = {}, {}, {}, {}
 
         def form_dz(b, g, squares, dy_ts):
-            if (b, g) == (LAST, PASSES - 1):
-                neg_dz = place("neg_dz_last", [P, PASS], BF16, TAIL_LANE, 1.5)
-            else:
-                neg_dz = own("neg_dz%d_%d" % (b, g), [P, PASS], BF16)
+            neg_dz = own("neg_dz%d_%d" % (b, g), [P, PASS], BF16)
             nc.vector.scalar_tensor_tensor(neg_dz[:], squares[:, pass_slots[g]], 1.0, dy_ts[:], ALU.subtract, ALU.mult)
             pairs = neg_dz[:].bitcast(F32).rearrange("n (p u) -> n u p", u=2)
-            if g == 0 or b == LAST:
+            if g == 0:
                 dz_banks[b, g] = psum.tile([P, PASSES, 2, P], F32, name="dz_bank", bufs=2)
-            bank = dz_banks[b, g][:, 0] if b == LAST else dz_banks[b, 0][:, g]
+            bank = dz_banks[b, 0][:, g]
             for u in range(2):
                 nc.tensor.transpose(bank[:, u, :], pairs[:, u, :], ident[:])
 
-        def fetch_dz(b, passes, tile):
+        def fetch_dz(b, passes, tile, copy):
             n = len(passes)
-            nc.scalar.copy(
+            copy(
                 tile[:].bitcast(F32).rearrange("p (g n u) -> p g n u", g=n, u=2),
-                dz_banks[b, passes[0]][:, 0:n].rearrange("p g u n -> p g n u"),
+                dz_banks[b, 0][:, passes[0] : passes[0] + n].rearrange("p g u n -> p g n u"),
             )
             for i, g in enumerate(passes):
                 dz_turned[b, g] = tile[:, pass_slots[i]]
@@ -135,10 +144,9 @@ def tile_attend_gex_tnh_w_kernel(tc, xT, dyT, hT, ts, offs, out):
                 x_banks[b][:].rearrange("p g u d -> p g d u"),
             )
 
-        def quantize_x(b, codes):
-            x_codes[b] = codes
-            x_scales[b] = own("x_scales%d" % b, [P, PASSES * P], U8)
-            nc.vector.quantize_mx(out=codes[:].bitcast(E4M3), scales=x_scales[b][:], in_=x_turned[b])
+        def quantize_x(b, codes, scales):
+            x_codes[b], x_scales[b] = codes, scales
+            nc.vector.quantize_mx(out=codes.bitcast(E4M3), scales=scales, in_=x_turned[b])
 
         accs = [psum.tile([P, DV], F32, name="acc", bufs=BLOCKS) for b in range(BLOCKS)]
 
@@ -153,19 +161,44 @@ def tile_attend_gex_tnh_w_kernel(tc, xT, dyT, hT, ts, offs, out):
                 stop=(g == PASSES - 1),
             )
 
+        def warm_up(g):
+            nc.tensor.matmul_mx(
+                out=accs[LAST - g][:],
+                lhsT=dz_codes[0][:, rows(2 * g)].bitcast(E5M2),
+                lhsT_scale=dz_scales[0][:, rows(2 * g)],
+                rhs=first_codes[:].bitcast(E4M3),
+                rhs_scale=first_scales[:],
+                start=True,
+                stop=True,
+            )
+
         def store(b):
             result = own("result%d" % b, [P, DV], F32)
-            if b % 2 == 1:
+            if b % 2 == 0:
                 nc.scalar.activation(result[:], accs[b][:], ACT.Copy, scale=-1.0)
             else:
                 nc.vector.tensor_scalar_mul(result[:], accs[b][:], -1.0)
             nc.sync.dma_start(out[0, rows(b), :], result[:])
 
+        def cast_x(b, i, x_win):
+            nc.scalar.activation(x_win[:, x_pieces[b][i]], x_raw[b, i][:], ACT.Copy)
+
+        def gather_dy(b, g, dy_ts):
+            nc.vector.tensor_tensor(dy_ts[:], dy_win[b][:].indirect(pass_lists[g]), ts_got[g][:], ALU.mult)
+
+        def square(b, h_got, squares):
+            for g in range(PASSES):
+                nc.scalar.activation(squares[:, pass_slots[g]], h_got[:, pass_slots[g]], ACT.Square)
+
+        width = PASSES * P
+        first_codes = place("x_codes01", [P, 2 * width], U32, 1, 5)
+        first_scales = own("x_scales01", [P, 2 * width], U8)
+
         all_passes = tuple(range(PASSES))
-        for b in range(BLOCKS):
+        for b in range(LAST):
             x_win = place("x_win%d" % b, [P, TOKENS], BF16, X_LANE + b, 2)
             for half in range(2):
-                nc.scalar.activation(x_win[:, token_halves[half]], x_raw[b, half][:], ACT.Copy)
+                cast_x(b, half, x_win)
             if b == 2:
                 fetch_x(b - 1, own("x_raw%d_0" % b, [P, SLOTS], BF16)[:])
 
@@ -176,42 +209,63 @@ def tile_attend_gex_tnh_w_kernel(tc, xT, dyT, hT, ts, offs, out):
             nc.vector.tensor_copy(h_got[:], h_win[b][:].indirect(offsets[:]))
             if b == 0:
                 for g in range(PASSES):
-                    nc.vector.tensor_copy(ts_got[:, pass_slots[g]], ts_win[:].indirect(pass_lists[g]))
-            if b >= 2:
-                quantize_x(b - 2, place("x_codes%d" % (b - 2), [P, PASSES * P], U32, b - 1, 5))
+                    nc.vector.tensor_copy(ts_got[g][:], ts_win[:].indirect(pass_lists[g]))
+            if b == 2:
+                for i in range(2):
+                    cols = slice(i * width, (i + 1) * width)
+                    quantize_x(i, first_codes[:, cols], first_scales[:, cols])
 
-            if b < LAST:
-                x_got = place("x_got%d" % b, [P, SLOTS], BF16, X_LANE + b + 1, 5)
-            else:
-                x_got = own("x_got%d" % b, [P, SLOTS], BF16)
+            x_got = place("x_got%d" % b, [P, SLOTS], BF16, X_LANE + b + 1, 5)
             gather_x(b, x_win, x_got)
             squares = place("squares%d" % b, [P, SLOTS], F32, b + 1, 4)
-            for g in range(PASSES):
-                nc.scalar.activation(squares[:, pass_slots[g]], h_got[:, pass_slots[g]], ACT.Square)
+            square(b, h_got, squares)
             if b == 0:
                 fetch_x(b, own("x_turned0", [P, SLOTS], BF16)[:])
             else:
-                fetch_dz(b - 1, all_passes, place("dz_turned%d" % (b - 1), [P, SLOTS], BF16, X_LANE + b, 2))
+                turned = place("dz_turned%d" % (b - 1), [P, SLOTS], BF16, X_LANE + b, 2)
+                fetch_dz(b - 1, all_passes, turned, nc.scalar.copy)
+            if b == 2:
+                fetch_x(b, own("x_turned2", [P, SLOTS], BF16)[:])
+                last_h = own("h_got%d" % LAST, [P, SLOTS], F32)
+                nc.vector.tensor_copy(last_h[:], h_win[LAST][:].indirect(offsets[:]))
+                last_squares = own("squares%d" % LAST, [P, SLOTS], F32)
+                square(LAST, last_h, last_squares)
 
             dy_ts = [place("dy_ts%d_%d" % (b, g), [P, PASS], F32, b, 4 + 2 * g) for g in range(PASSES)]
             for g in range(PASSES):
-                gathered = dy_win[b][:].indirect(pass_lists[g])
-                nc.vector.tensor_tensor(dy_ts[g][:], gathered, ts_got[:, pass_slots[g]], ALU.mult)
+                gather_dy(b, g, dy_ts[g])
             for g in range(PASSES):
                 form_dz(b, g, squares, dy_ts[g])
 
-        for g, (lane, kib) in enumerate(((LAST, 3), (TAIL_LANE, 0))):
-            dz_codes[g] = place("dz_codes%d" % g, [P, DV], U32, lane, kib)
-            for b in range(LAST):
-                quantize_dz(b, g)
-            fetch_dz(LAST, (g,), own("dz_turned%d_%d" % (LAST, g), [P, PASS], BF16))
+        x_win = place("x_win%d" % LAST, [P, TOKENS], BF16, X_LANE + LAST, 2)
+        cast_x(LAST, 0, x_win)
+        squares = last_squares
+        cast_x(LAST, 1, x_win)
+        cast_x(LAST, 2, x_win)
+
+        dy_ts = [place("dy_ts_last%d" % g, [P, PASS], F32, LAST, 4 + 2 * g) for g in range(PASSES)]
+        for g in range(PASSES):
+            gather_dy(LAST, g, dy_ts[g])
+        gather_x(LAST, x_win, own("x_got%d" % LAST, [P, SLOTS], BF16))
+        form_dz(LAST, 0, squares, dy_ts[0])
+        dz_codes[0] = place("dz_codes0", [P, DV], U32, TAIL_LANE, 18)
+        for b in range(LAST - 1):
+            quantize_dz(b, 0)
+        warm_up(0)
+        form_dz(LAST, 1, squares, dy_ts[1])
+        quantize_x(2, place("x_codes2", [P, width], U32, TAIL_LANE, 23)[:], own("x_scales2", [P, width], U8)[:])
+        dz_codes[1] = place("dz_codes1", [P, DV], U32, TAIL_LANE, 20.5)
+        for b in range(LAST - 1):
+            quantize_dz(b, 1)
+        fetch_dz(LAST - 1, all_passes, place("dz_turned2", [P, SLOTS], BF16, TAIL_LANE, 12.5), nc.scalar.copy)
+        for g in range(PASSES):
+            quantize_dz(LAST - 1, g)
+        warm_up(1)
+        for g in range(PASSES):
+            fetch_dz(LAST, (g,), place("dz_turned3_%d" % g, [P, PASS], BF16, TAIL_LANE, 14.5 + g), nc.scalar.copy)
             quantize_dz(LAST, g)
-
-        late = place("late_turned", [P, 2, SLOTS], BF16, TAIL_LANE, 2)
-        for i, b in enumerate((LAST - 1, LAST)):
-            fetch_x(b, late[:, i])
-            quantize_x(b, own("x_codes%d" % b, [P, PASSES * P], U32))
-
+        fetch_x(LAST, own("x_turned3", [P, SLOTS], BF16)[:])
+        quantize_x(LAST, own("x_codes3", [P, width], U32)[:], own("x_scales3", [P, width], U8)[:])
         multiply(0, 0)
         multiply(1, 0)
         for b in range(BLOCKS):

@@ -71,19 +71,21 @@ def tile_attend_gex_tnh_w_kernel(tc, xT, dyT, hT, ts, offs, out):
         for b in range(LAST):
             x_pieces[b] = token_halves
             x_raw[b, 0] = own("x_raw%d_0" % b, [P, TOKENS // 2], F32)
-            x_raw[b, 1] = place("x_raw%d_1" % b, [P, TOKENS // 2], F32, b + 1, 4)
+            if b == 1:
+                x_raw[b, 1] = place("x_raw%d_1" % b, [P, TOKENS // 2], F32, b + 1, 4)
+            else:
+                x_raw[b, 1] = own("x_raw%d_1" % b, [P, TOKENS // 2], F32)
         x_pieces[LAST] = [slice(0, 1024), slice(1024, 1536), slice(1536, 2048)]
-        x_raw[LAST, 0] = place("x_raw_last0", [P, 1024], F32, TAIL_LANE, 4)
+        x_raw[LAST, 0] = place("x_raw_last0", [P, 1024], F32, TAIL_LANE, 0)
         x_raw[LAST, 1] = own("x_raw_last1", [P, 512], F32)
-        x_raw[LAST, 2] = place("x_raw_last2", [P, 512], F32, TAIL_LANE, 14)
+        x_raw[LAST, 2] = place("x_raw_last2", [P, 512], F32, TAIL_LANE, 5)
 
         for b in range(BLOCKS):
             if b < LAST:
                 nc.sync.dma_start(h_win[b][:], hT[rows(b), :])
             if b == 0:
                 nc.sync.dma_start(offsets[:], offs)
-            early = 2 if b < LAST else 1
-            for i, piece in enumerate(x_pieces[b][:early]):
+            for i, piece in enumerate(x_pieces[b][: 2 if b < LAST else 1]):
                 nc.sync.dma_start(x_raw[b, i][:], xT[rows(b), piece])
             if b == LAST - 1:
                 nc.sync.dma_start(h_win[LAST][:], hT[rows(LAST), :])
@@ -100,7 +102,7 @@ def tile_attend_gex_tnh_w_kernel(tc, xT, dyT, hT, ts, offs, out):
                 nc.tensor.transpose(spread[:, j, :], ts_cols[:, col : col + 1].to_broadcast([P, P]), ident[:])
             nc.scalar.copy(ts_view[:, :, BANK_COLS * c : BANK_COLS * (c + 1)], spread[:].rearrange("m j p -> m p j"))
 
-        ts_got = [place("ts_got0", [P, PASS], F32, TAIL_LANE, 18), place("ts_got1", [P, PASS], F32, TAIL_LANE, 22)]
+        ts_got = [place("ts_got0", [P, PASS], F32, TAIL_LANE, 12), place("ts_got1", [P, PASS], F32, TAIL_LANE, 14)]
         dz_scales = [own("dz_scales%d" % g, [P, DV], U8) for g in range(PASSES)]
         dz_banks, dz_turned, dz_codes = {}, {}, {}
         x_banks, x_turned, x_codes, x_scales = {}, {}, {}, {}
@@ -109,9 +111,14 @@ def tile_attend_gex_tnh_w_kernel(tc, xT, dyT, hT, ts, offs, out):
             neg_dz = own("neg_dz%d_%d" % (b, g), [P, PASS], BF16)
             nc.vector.scalar_tensor_tensor(neg_dz[:], squares[:, pass_slots[g]], 1.0, dy_ts[:], ALU.subtract, ALU.mult)
             pairs = neg_dz[:].bitcast(F32).rearrange("n (p u) -> n u p", u=2)
-            if g == 0:
-                dz_banks[b, g] = psum.tile([P, PASSES, 2, P], F32, name="dz_bank", bufs=2)
-            bank = dz_banks[b, 0][:, g]
+            if b < 2:
+                if g == 0:
+                    dz_banks[b, g] = psum.tile([P, PASSES, 2, P], F32, name=("bank_c", "bank_b")[b])
+                bank = dz_banks[b, 0][:, g]
+            else:
+                if b == 2:
+                    dz_banks[b, g] = psum.tile([P, 2, 2, P], F32, name=("bank_a", "bank_b")[g])
+                bank = dz_banks[2, g][:, b - 2]
             for u in range(2):
                 nc.tensor.transpose(bank[:, u, :], pairs[:, u, :], ident[:])
 
@@ -119,7 +126,7 @@ def tile_attend_gex_tnh_w_kernel(tc, xT, dyT, hT, ts, offs, out):
             n = len(passes)
             copy(
                 tile[:].bitcast(F32).rearrange("p (g n u) -> p g n u", g=n, u=2),
-                dz_banks[b, 0][:, passes[0] : passes[0] + n].rearrange("p g u n -> p g n u"),
+                dz_banks[b, passes[0]][:, 0:n].rearrange("p g u n -> p g n u"),
             )
             for i, g in enumerate(passes):
                 dz_turned[b, g] = tile[:, pass_slots[i]]
@@ -132,7 +139,7 @@ def tile_attend_gex_tnh_w_kernel(tc, xT, dyT, hT, ts, offs, out):
             laid = x_got[:].rearrange("d (u r e) -> d r u e", u=2, e=2)
             nc.scalar.activation(laid, x_win[:].indirect(offsets[:]), ACT.Copy)
             pairs = x_got[:].bitcast(F32).rearrange("d (u g p) -> d g u p", g=PASSES, u=2)
-            x_banks[b] = psum.tile([P, PASSES, 2, P], F32, name="x_bank", bufs=2)
+            x_banks[b] = psum.tile([P, PASSES, 2, P], F32, name=("bank_c", "bank_d")[b % 2])
             for g in range(PASSES):
                 for u in range(2):
                     nc.tensor.transpose(x_banks[b][:, g, u, :], pairs[:, g, u, :], ident[:])
@@ -161,17 +168,6 @@ def tile_attend_gex_tnh_w_kernel(tc, xT, dyT, hT, ts, offs, out):
                 stop=(g == PASSES - 1),
             )
 
-        def warm_up(g):
-            nc.tensor.matmul_mx(
-                out=accs[LAST - g][:],
-                lhsT=dz_codes[0][:, rows(2 * g)].bitcast(E5M2),
-                lhsT_scale=dz_scales[0][:, rows(2 * g)],
-                rhs=first_codes[:].bitcast(E4M3),
-                rhs_scale=first_scales[:],
-                start=True,
-                stop=True,
-            )
-
         def store(b):
             result = own("result%d" % b, [P, DV], F32)
             if b % 2 == 0:
@@ -191,8 +187,6 @@ def tile_attend_gex_tnh_w_kernel(tc, xT, dyT, hT, ts, offs, out):
                 nc.scalar.activation(squares[:, pass_slots[g]], h_got[:, pass_slots[g]], ACT.Square)
 
         width = PASSES * P
-        first_codes = place("x_codes01", [P, 2 * width], U32, 1, 5)
-        first_scales = own("x_scales01", [P, 2 * width], U8)
 
         all_passes = tuple(range(PASSES))
         for b in range(LAST):
@@ -211,16 +205,20 @@ def tile_attend_gex_tnh_w_kernel(tc, xT, dyT, hT, ts, offs, out):
                 for g in range(PASSES):
                     nc.vector.tensor_copy(ts_got[g][:], ts_win[:].indirect(pass_lists[g]))
             if b == 2:
-                for i in range(2):
-                    cols = slice(i * width, (i + 1) * width)
-                    quantize_x(i, first_codes[:, cols], first_scales[:, cols])
+                quantize_x(0, place("x_codes0", [P, width], U32, 1, 5)[:], own("x_scales0", [P, width], U8)[:])
 
             x_got = place("x_got%d" % b, [P, SLOTS], BF16, X_LANE + b + 1, 5)
             gather_x(b, x_win, x_got)
-            squares = place("squares%d" % b, [P, SLOTS], F32, b + 1, 4)
-            square(b, h_got, squares)
+            if b == 2:
+                squares = place("squares%d" % b, [P, SLOTS], F32, TAIL_LANE, 17)
+            else:
+                squares = place("squares%d" % b, [P, SLOTS], F32, b + 1, 4)
+            if b == 1:
+                square(b, h_got, squares)
+            else:
+                nc.gpsimd.tensor_tensor(squares[:], h_got[:], h_got[:], ALU.mult)
             if b == 0:
-                fetch_x(b, own("x_turned0", [P, SLOTS], BF16)[:])
+                fetch_x(b, place("x_turned0", [P, SLOTS], BF16, TAIL_LANE, 16)[:])
             else:
                 turned = place("dz_turned%d" % (b - 1), [P, SLOTS], BF16, X_LANE + b, 2)
                 fetch_dz(b - 1, all_passes, turned, nc.scalar.copy)
@@ -231,39 +229,40 @@ def tile_attend_gex_tnh_w_kernel(tc, xT, dyT, hT, ts, offs, out):
                 last_squares = own("squares%d" % LAST, [P, SLOTS], F32)
                 square(LAST, last_h, last_squares)
 
-            dy_ts = [place("dy_ts%d_%d" % (b, g), [P, PASS], F32, b, 4 + 2 * g) for g in range(PASSES)]
-            for g in range(PASSES):
-                gather_dy(b, g, dy_ts[g])
-            for g in range(PASSES):
-                form_dz(b, g, squares, dy_ts[g])
+            if b < LAST:
+                dy_ts = [place("dy_ts%d_%d" % (b, g), [P, PASS], F32, b, 4 + 2 * g) for g in range(PASSES)]
+                for g in range(PASSES):
+                    gather_dy(b, g, dy_ts[g])
+                for g in range(PASSES):
+                    form_dz(b, g, squares, dy_ts[g])
+
+        def close_late(g, turned):
+            nc.scalar.copy(
+                turned[:].bitcast(F32).rearrange("p (b n u) -> p b n u", b=2, u=2),
+                dz_banks[2, g][:].rearrange("p b u n -> p b n u"),
+            )
+            cols = slice(2 * P, 4 * P)
+            nc.vector.quantize_mx(out=dz_codes[g][:, cols].bitcast(E5M2), scales=dz_scales[g][:, cols], in_=turned[:])
 
         x_win = place("x_win%d" % LAST, [P, TOKENS], BF16, X_LANE + LAST, 2)
-        cast_x(LAST, 0, x_win)
-        squares = last_squares
-        cast_x(LAST, 1, x_win)
-        cast_x(LAST, 2, x_win)
-
-        dy_ts = [place("dy_ts_last%d" % g, [P, PASS], F32, LAST, 4 + 2 * g) for g in range(PASSES)]
+        for i in range(3):
+            cast_x(LAST, i, x_win)
+        dy_ts = [place("dy_ts3_%d" % g, [P, PASS], F32, TAIL_LANE, (19, 17)[g]) for g in range(PASSES)]
         for g in range(PASSES):
             gather_dy(LAST, g, dy_ts[g])
         gather_x(LAST, x_win, own("x_got%d" % LAST, [P, SLOTS], BF16))
-        form_dz(LAST, 0, squares, dy_ts[0])
-        dz_codes[0] = place("dz_codes0", [P, DV], U32, TAIL_LANE, 18)
-        for b in range(LAST - 1):
+        form_dz(LAST, 0, last_squares, dy_ts[0])
+        dz_codes[0] = place("dz_codes0", [P, DV], U32, TAIL_LANE, 12)
+        for b in range(2):
             quantize_dz(b, 0)
-        warm_up(0)
-        form_dz(LAST, 1, squares, dy_ts[1])
-        quantize_x(2, place("x_codes2", [P, width], U32, TAIL_LANE, 23)[:], own("x_scales2", [P, width], U8)[:])
-        dz_codes[1] = place("dz_codes1", [P, DV], U32, TAIL_LANE, 20.5)
-        for b in range(LAST - 1):
+        form_dz(LAST, 1, last_squares, dy_ts[1])
+        quantize_x(1, own("x_codes1", [P, width], U32)[:], place("x_scales1", [P, width], U8, TAIL_LANE, 14)[:])
+        close_late(0, place("dz_late0", [P, SLOTS], BF16, TAIL_LANE, 3.5))
+        dz_codes[1] = place("dz_codes1", [P, DV], U32, TAIL_LANE, 2)
+        for b in range(2):
             quantize_dz(b, 1)
-        fetch_dz(LAST - 1, all_passes, place("dz_turned2", [P, SLOTS], BF16, TAIL_LANE, 12.5), nc.scalar.copy)
-        for g in range(PASSES):
-            quantize_dz(LAST - 1, g)
-        warm_up(1)
-        for g in range(PASSES):
-            fetch_dz(LAST, (g,), place("dz_turned3_%d" % g, [P, PASS], BF16, TAIL_LANE, 14.5 + g), nc.scalar.copy)
-            quantize_dz(LAST, g)
+        close_late(1, place("dz_late1", [P, SLOTS], BF16, TAIL_LANE, 6))
+        quantize_x(2, own("x_codes2", [P, width], U32)[:], place("x_scales2", [P, width], U8, TAIL_LANE, 6)[:])
         fetch_x(LAST, own("x_turned3", [P, SLOTS], BF16)[:])
         quantize_x(LAST, own("x_codes3", [P, width], U32)[:], own("x_scales3", [P, width], U8)[:])
         multiply(0, 0)

@@ -59,39 +59,48 @@ def tile_attend_gex_tnh_w_kernel(tc, xT, dyT, hT, ts, offs, out):
         nc.sync.dma_start(ts_cols[:], ts[0, :].rearrange("(p j) -> p j", p=P))
         pass_lists = [offsets[:, g * LIST_COLS : (g + 1) * LIST_COLS] for g in range(PASSES)]
         pass_slots = [slice(g * PASS, (g + 1) * PASS) for g in range(PASSES)]
-        token_halves = [slice(0, TOKENS // 2), slice(TOKENS // 2, TOKENS)]
 
         ident = keep.tile([P, P], F32, name="ident")
         make_identity(nc, ident[:])
 
         h_win = [own("h_win%d" % b, [P, TOKENS], F32) for b in range(BLOCKS)]
         dy_win = [own("dy_win%d" % b, [P, TOKENS], F32) for b in range(BLOCKS)]
-        x_raw = {}
-        x_pieces = {}
-        for b in range(LAST):
-            x_pieces[b] = token_halves
-            x_raw[b, 0] = own("x_raw%d_0" % b, [P, TOKENS // 2], F32)
-            if b == 1:
-                x_raw[b, 1] = place("x_raw%d_1" % b, [P, TOKENS // 2], F32, b + 1, 4)
-            else:
-                x_raw[b, 1] = own("x_raw%d_1" % b, [P, TOKENS // 2], F32)
-        x_pieces[LAST] = [slice(0, 1024), slice(1024, 1536), slice(1536, 2048)]
-        x_raw[LAST, 0] = place("x_raw_last0", [P, 1024], F32, TAIL_LANE, 0)
-        x_raw[LAST, 1] = own("x_raw_last1", [P, 512], F32)
-        x_raw[LAST, 2] = place("x_raw_last2", [P, 512], F32, TAIL_LANE, 5)
 
-        for b in range(BLOCKS):
-            if b < LAST:
-                nc.sync.dma_start(h_win[b][:], hT[rows(b), :])
+        half, quarter = TOKENS // 2, TOKENS // 4
+        x_pieces, x_raw = {}, {}
+        for b in range(LAST):
+            x_pieces[b] = [slice(0, half), slice(half, TOKENS)]
+            x_raw[b, 0] = own("x_raw%d_0" % b, [P, half], F32)
+            if b == 1:
+                x_raw[b, 1] = place("x_raw%d_1" % b, [P, half], F32, b + 1, 4)
+            else:
+                x_raw[b, 1] = own("x_raw%d_1" % b, [P, half], F32)
+        x_pieces[LAST] = [slice(0, half), slice(half, half + quarter), slice(half + quarter, TOKENS)]
+        x_raw[LAST, 0] = place("x_raw_last0", [P, half], F32, TAIL_LANE, 0)
+        x_raw[LAST, 1] = own("x_raw_last1", [P, quarter], F32)
+        x_raw[LAST, 2] = place("x_raw_last2", [P, quarter], F32, TAIL_LANE, 5)
+
+        def load_h(b):
+            nc.sync.dma_start(h_win[b][:], hT[rows(b), :])
+
+        def load_dy(b):
+            nc.sync.dma_start(dy_win[b][:], dyT[rows(b), :])
+
+        def load_x(b, *pieces):
+            for i in pieces:
+                nc.sync.dma_start(x_raw[b, i][:], xT[rows(b), x_pieces[b][i]])
+
+        for b in range(LAST):
+            load_h(b)
             if b == 0:
                 nc.sync.dma_start(offsets[:], offs)
-            for i, piece in enumerate(x_pieces[b][: 2 if b < LAST else 1]):
-                nc.sync.dma_start(x_raw[b, i][:], xT[rows(b), piece])
+            load_x(b, 0, 1)
             if b == LAST - 1:
-                nc.sync.dma_start(h_win[LAST][:], hT[rows(LAST), :])
-            nc.sync.dma_start(dy_win[b][:], dyT[rows(b), :])
-        for i in (1, 2):
-            nc.sync.dma_start(x_raw[LAST, i][:], xT[rows(LAST), x_pieces[LAST][i]])
+                load_h(LAST)
+            load_dy(b)
+        load_x(LAST, 0)
+        load_dy(LAST)
+        load_x(LAST, 1, 2)
 
         ts_win = own("ts_win", [P, TOKENS], F32)
         ts_view = ts_win[:].rearrange("m (p j) -> m p j", p=P)
@@ -102,15 +111,35 @@ def tile_attend_gex_tnh_w_kernel(tc, xT, dyT, hT, ts, offs, out):
                 nc.tensor.transpose(spread[:, j, :], ts_cols[:, col : col + 1].to_broadcast([P, P]), ident[:])
             nc.scalar.copy(ts_view[:, :, BANK_COLS * c : BANK_COLS * (c + 1)], spread[:].rearrange("m j p -> m p j"))
 
-        ts_got = [place("ts_got0", [P, PASS], F32, TAIL_LANE, 12), place("ts_got1", [P, PASS], F32, TAIL_LANE, 14)]
+        ts_got = [place("ts_got%d" % g, [P, PASS], F32, TAIL_LANE, 12 + 2 * g) for g in range(PASSES)]
         dz_scales = [own("dz_scales%d" % g, [P, DV], U8) for g in range(PASSES)]
         dz_banks, dz_turned, dz_codes = {}, {}, {}
         x_banks, x_turned, x_codes, x_scales = {}, {}, {}, {}
 
+        def gather_h(b, h_got):
+            nc.vector.tensor_copy(h_got[:], h_win[b][:].indirect(offsets[:]))
+
+        def gather_dy(b, g, dy_ts):
+            nc.vector.tensor_tensor(dy_ts[:], dy_win[b][:].indirect(pass_lists[g]), ts_got[g][:], ALU.mult)
+
+        def square(h_got, squares):
+            for g in range(PASSES):
+                nc.scalar.activation(squares[:, pass_slots[g]], h_got[:, pass_slots[g]], ACT.Square)
+
         def form_dz(b, g, squares, dy_ts):
             neg_dz = own("neg_dz%d_%d" % (b, g), [P, PASS], BF16)
-            nc.vector.scalar_tensor_tensor(neg_dz[:], squares[:, pass_slots[g]], 1.0, dy_ts[:], ALU.subtract, ALU.mult)
-            pairs = neg_dz[:].bitcast(F32).rearrange("n (p u) -> n u p", u=2)
+            if b < LAST:
+                nc.vector.scalar_tensor_tensor(
+                    neg_dz[:], squares[:, pass_slots[g]], 1.0, dy_ts[:], ALU.subtract, ALU.mult
+                )
+                pairs = neg_dz[:].bitcast(F32).rearrange("n (p u) -> n u p", u=2)
+            else:
+                laid = neg_dz[:].rearrange("n (u p e) -> n u p e", u=2, e=2)
+                in0 = squares[:, pass_slots[g]].rearrange("n (p u e) -> n u p e", u=2, e=2)
+                in1 = dy_ts[:].rearrange("n (p u e) -> n u p e", u=2, e=2)
+                for u in range(2):
+                    nc.vector.scalar_tensor_tensor(laid[:, u], in0[:, u], 1.0, in1[:, u], ALU.subtract, ALU.mult)
+                pairs = neg_dz[:].bitcast(F32).rearrange("n (u p) -> n u p", u=2)
             if b < 2:
                 if g == 0:
                     dz_banks[b, g] = psum.tile([P, PASSES, 2, P], F32, name=("bank_c", "bank_b")[b])
@@ -122,18 +151,29 @@ def tile_attend_gex_tnh_w_kernel(tc, xT, dyT, hT, ts, offs, out):
             for u in range(2):
                 nc.tensor.transpose(bank[:, u, :], pairs[:, u, :], ident[:])
 
-        def fetch_dz(b, passes, tile, copy):
-            n = len(passes)
-            copy(
-                tile[:].bitcast(F32).rearrange("p (g n u) -> p g n u", g=n, u=2),
-                dz_banks[b, passes[0]][:, 0:n].rearrange("p g u n -> p g n u"),
+        def fetch_dz(b, turned):
+            nc.scalar.copy(
+                turned[:].bitcast(F32).rearrange("p (g n u) -> p g n u", g=PASSES, u=2),
+                dz_banks[b, 0][:].rearrange("p g u n -> p g n u"),
             )
-            for i, g in enumerate(passes):
-                dz_turned[b, g] = tile[:, pass_slots[i]]
+            for g in range(PASSES):
+                dz_turned[b, g] = turned[:, pass_slots[g]]
 
         def quantize_dz(b, g):
             codes = dz_codes[g][:, rows(b)].bitcast(E5M2)
             nc.vector.quantize_mx(out=codes, scales=dz_scales[g][:, rows(b)], in_=dz_turned[b, g])
+
+        def close_pass(g, turned):
+            nc.scalar.copy(
+                turned[:].bitcast(F32).rearrange("p (b n u) -> p b n u", b=2, u=2),
+                dz_banks[2, g][:].rearrange("p b u n -> p b n u"),
+            )
+            cols = slice(2 * P, 4 * P)
+            nc.vector.quantize_mx(out=dz_codes[g][:, cols].bitcast(E5M2), scales=dz_scales[g][:, cols], in_=turned[:])
+
+        def cast_x(b, x_win):
+            for i, piece in enumerate(x_pieces[b]):
+                nc.scalar.activation(x_win[:, piece], x_raw[b, i][:], ACT.Copy)
 
         def gather_x(b, x_win, x_got):
             laid = x_got[:].rearrange("d (u r e) -> d r u e", u=2, e=2)
@@ -147,13 +187,15 @@ def tile_attend_gex_tnh_w_kernel(tc, xT, dyT, hT, ts, offs, out):
         def fetch_x(b, turned):
             x_turned[b] = turned
             nc.scalar.copy(
-                turned.bitcast(F32).rearrange("p (g d u) -> p g d u", g=PASSES, u=2),
+                turned[:].bitcast(F32).rearrange("p (g d u) -> p g d u", g=PASSES, u=2),
                 x_banks[b][:].rearrange("p g u d -> p g d u"),
             )
 
+        x_width = PASSES * P
+
         def quantize_x(b, codes, scales):
             x_codes[b], x_scales[b] = codes, scales
-            nc.vector.quantize_mx(out=codes.bitcast(E4M3), scales=scales, in_=x_turned[b])
+            nc.vector.quantize_mx(out=codes[:].bitcast(E4M3), scales=scales[:], in_=x_turned[b][:])
 
         accs = [psum.tile([P, DV], F32, name="acc", bufs=BLOCKS) for b in range(BLOCKS)]
 
@@ -176,95 +218,72 @@ def tile_attend_gex_tnh_w_kernel(tc, xT, dyT, hT, ts, offs, out):
                 nc.vector.tensor_scalar_mul(result[:], accs[b][:], -1.0)
             nc.sync.dma_start(out[0, rows(b), :], result[:])
 
-        def cast_x(b, i, x_win):
-            nc.scalar.activation(x_win[:, x_pieces[b][i]], x_raw[b, i][:], ACT.Copy)
-
-        def gather_dy(b, g, dy_ts):
-            nc.vector.tensor_tensor(dy_ts[:], dy_win[b][:].indirect(pass_lists[g]), ts_got[g][:], ALU.mult)
-
-        def square(b, h_got, squares):
-            for g in range(PASSES):
-                nc.scalar.activation(squares[:, pass_slots[g]], h_got[:, pass_slots[g]], ACT.Square)
-
-        width = PASSES * P
-
-        all_passes = tuple(range(PASSES))
         for b in range(LAST):
             x_win = place("x_win%d" % b, [P, TOKENS], BF16, X_LANE + b, 2)
-            for half in range(2):
-                cast_x(b, half, x_win)
+            cast_x(b, x_win)
             if b == 2:
-                fetch_x(b - 1, own("x_raw%d_0" % b, [P, SLOTS], BF16)[:])
+                fetch_x(b - 1, own("x_raw%d_0" % b, [P, SLOTS], BF16))
 
             if b == 0:
                 h_got = own("h_got0", [P, SLOTS], F32)
             else:
                 h_got = place("h_got%d" % b, [P, SLOTS], F32, b - 1, 1)
-            nc.vector.tensor_copy(h_got[:], h_win[b][:].indirect(offsets[:]))
+            gather_h(b, h_got)
             if b == 0:
                 for g in range(PASSES):
                     nc.vector.tensor_copy(ts_got[g][:], ts_win[:].indirect(pass_lists[g]))
             if b == 2:
-                quantize_x(0, place("x_codes0", [P, width], U32, 1, 5)[:], own("x_scales0", [P, width], U8)[:])
+                quantize_x(0, place("x_codes0", [P, x_width], U32, 1, 5), own("x_scales0", [P, x_width], U8))
 
-            x_got = place("x_got%d" % b, [P, SLOTS], BF16, X_LANE + b + 1, 5)
-            gather_x(b, x_win, x_got)
+            gather_x(b, x_win, place("x_got%d" % b, [P, SLOTS], BF16, X_LANE + b + 1, 5))
             if b == 2:
                 squares = place("squares%d" % b, [P, SLOTS], F32, TAIL_LANE, 17)
             else:
                 squares = place("squares%d" % b, [P, SLOTS], F32, b + 1, 4)
             if b == 1:
-                square(b, h_got, squares)
+                square(h_got, squares)
             else:
                 nc.gpsimd.tensor_tensor(squares[:], h_got[:], h_got[:], ALU.mult)
             if b == 0:
-                fetch_x(b, place("x_turned0", [P, SLOTS], BF16, TAIL_LANE, 16)[:])
+                fetch_x(b, place("x_turned0", [P, SLOTS], BF16, TAIL_LANE, 16))
             else:
-                turned = place("dz_turned%d" % (b - 1), [P, SLOTS], BF16, X_LANE + b, 2)
-                fetch_dz(b - 1, all_passes, turned, nc.scalar.copy)
+                fetch_dz(b - 1, place("dz_turned%d" % (b - 1), [P, SLOTS], BF16, X_LANE + b, 2))
             if b == 2:
-                fetch_x(b, own("x_turned2", [P, SLOTS], BF16)[:])
+                fetch_x(b, own("x_turned2", [P, SLOTS], BF16))
                 last_h = own("h_got%d" % LAST, [P, SLOTS], F32)
-                nc.vector.tensor_copy(last_h[:], h_win[LAST][:].indirect(offsets[:]))
+                gather_h(LAST, last_h)
                 last_squares = own("squares%d" % LAST, [P, SLOTS], F32)
-                square(LAST, last_h, last_squares)
+                square(last_h, last_squares)
 
-            if b < LAST:
-                dy_ts = [place("dy_ts%d_%d" % (b, g), [P, PASS], F32, b, 4 + 2 * g) for g in range(PASSES)]
-                for g in range(PASSES):
-                    gather_dy(b, g, dy_ts[g])
-                for g in range(PASSES):
-                    form_dz(b, g, squares, dy_ts[g])
-
-        def close_late(g, turned):
-            nc.scalar.copy(
-                turned[:].bitcast(F32).rearrange("p (b n u) -> p b n u", b=2, u=2),
-                dz_banks[2, g][:].rearrange("p b u n -> p b n u"),
-            )
-            cols = slice(2 * P, 4 * P)
-            nc.vector.quantize_mx(out=dz_codes[g][:, cols].bitcast(E5M2), scales=dz_scales[g][:, cols], in_=turned[:])
+            dy_ts = [place("dy_ts%d_%d" % (b, g), [P, PASS], F32, b, 4 + 2 * g) for g in range(PASSES)]
+            for g in range(PASSES):
+                gather_dy(b, g, dy_ts[g])
+            for g in range(PASSES):
+                form_dz(b, g, squares, dy_ts[g])
 
         x_win = place("x_win%d" % LAST, [P, TOKENS], BF16, X_LANE + LAST, 2)
-        for i in range(3):
-            cast_x(LAST, i, x_win)
-        dy_ts = [place("dy_ts3_%d" % g, [P, PASS], F32, TAIL_LANE, (19, 17)[g]) for g in range(PASSES)]
+        cast_x(LAST, x_win)
+        dy_ts = [place("dy_ts3_%d" % g, [P, PASS], F32, TAIL_LANE, 19 - 2 * g) for g in range(PASSES)]
         for g in range(PASSES):
             gather_dy(LAST, g, dy_ts[g])
         gather_x(LAST, x_win, own("x_got%d" % LAST, [P, SLOTS], BF16))
+
         form_dz(LAST, 0, last_squares, dy_ts[0])
         dz_codes[0] = place("dz_codes0", [P, DV], U32, TAIL_LANE, 12)
         for b in range(2):
             quantize_dz(b, 0)
         form_dz(LAST, 1, last_squares, dy_ts[1])
-        quantize_x(1, own("x_codes1", [P, width], U32)[:], place("x_scales1", [P, width], U8, TAIL_LANE, 14)[:])
-        close_late(0, place("dz_late0", [P, SLOTS], BF16, TAIL_LANE, 3.5))
+        quantize_x(1, own("x_codes1", [P, x_width], U32), place("x_scales1", [P, x_width], U8, TAIL_LANE, 14))
+
+        close_pass(0, place("dz_late0", [P, SLOTS], BF16, TAIL_LANE, 3.5))
         dz_codes[1] = place("dz_codes1", [P, DV], U32, TAIL_LANE, 2)
         for b in range(2):
             quantize_dz(b, 1)
-        close_late(1, place("dz_late1", [P, SLOTS], BF16, TAIL_LANE, 6))
-        quantize_x(2, own("x_codes2", [P, width], U32)[:], place("x_scales2", [P, width], U8, TAIL_LANE, 6)[:])
-        fetch_x(LAST, own("x_turned3", [P, SLOTS], BF16)[:])
-        quantize_x(LAST, own("x_codes3", [P, width], U32)[:], own("x_scales3", [P, width], U8)[:])
+        close_pass(1, place("dz_late1", [P, SLOTS], BF16, TAIL_LANE, 6))
+        quantize_x(2, own("x_codes2", [P, x_width], U32), place("x_scales2", [P, x_width], U8, TAIL_LANE, 6))
+        fetch_x(LAST, own("x_turned3", [P, SLOTS], BF16))
+        quantize_x(LAST, own("x_codes3", [P, x_width], U32), own("x_scales3", [P, x_width], U8))
+
         multiply(0, 0)
         multiply(1, 0)
         for b in range(BLOCKS):

@@ -111,7 +111,7 @@ def tile_attend_gex_tnh_w_kernel(tc, xT, dyT, hT, ts, offs, out):
                 nc.tensor.transpose(spread[:, j, :], ts_cols[:, col : col + 1].to_broadcast([P, P]), ident[:])
             nc.scalar.copy(ts_view[:, :, BANK_COLS * c : BANK_COLS * (c + 1)], spread[:].rearrange("m j p -> m p j"))
 
-        ts_got = [place("ts_got%d" % g, [P, PASS], F32, TAIL_LANE, 12 + 2 * g) for g in range(PASSES)]
+        ts_got = [own("ts_got%d" % g, [P, PASS], F32) for g in range(PASSES)]
         dz_scales = [own("dz_scales%d" % g, [P, DV], U8) for g in range(PASSES)]
         dz_banks, dz_turned, dz_codes = {}, {}, {}
         x_banks, x_turned, x_codes, x_scales = {}, {}, {}, {}
@@ -211,12 +211,15 @@ def tile_attend_gex_tnh_w_kernel(tc, xT, dyT, hT, ts, offs, out):
             )
 
         def store(b):
-            result = own("result%d" % b, [P, DV], F32)
-            if b % 2 == 0:
-                nc.scalar.activation(result[:], accs[b][:], ACT.Copy, scale=-1.0)
-            else:
-                nc.vector.tensor_scalar_mul(result[:], accs[b][:], -1.0)
-            nc.sync.dma_start(out[0, rows(b), :], result[:])
+            pieces = 2 if b == LAST else 1
+            for i in range(pieces):
+                cols = slice(i * DV // pieces, (i + 1) * DV // pieces)
+                result = own("result%d_%d" % (b, i), [P, DV // pieces], F32)
+                if b % 2 == 0:
+                    nc.scalar.activation(result[:], accs[b][:, cols], ACT.Copy, scale=-1.0)
+                else:
+                    nc.vector.tensor_scalar_mul(result[:], accs[b][:, cols], -1.0)
+                nc.sync.dma_start(out[0, rows(b), cols], result[:])
 
         for b in range(LAST):
             x_win = place("x_win%d" % b, [P, TOKENS], BF16, X_LANE + b, 2)
@@ -268,12 +271,13 @@ def tile_attend_gex_tnh_w_kernel(tc, xT, dyT, hT, ts, offs, out):
             gather_dy(LAST, g, dy_ts[g])
         gather_x(LAST, x_win, own("x_got%d" % LAST, [P, SLOTS], BF16))
 
-        form_dz(LAST, 0, last_squares, dy_ts[0])
-        dz_codes[0] = place("dz_codes0", [P, DV], U32, TAIL_LANE, 12)
+        for g in range(PASSES):
+            form_dz(LAST, g, last_squares, dy_ts[g])
+
+        dz_codes[0] = place("dz_codes0", [P, DV], U32, TAIL_LANE, 20)
         for b in range(2):
             quantize_dz(b, 0)
-        form_dz(LAST, 1, last_squares, dy_ts[1])
-        quantize_x(1, own("x_codes1", [P, x_width], U32), place("x_scales1", [P, x_width], U8, TAIL_LANE, 14))
+        quantize_x(1, own("x_codes1", [P, x_width], U32), place("x_scales1", [P, x_width], U8, TAIL_LANE, 19))
 
         close_pass(0, place("dz_late0", [P, SLOTS], BF16, TAIL_LANE, 3.5))
         dz_codes[1] = place("dz_codes1", [P, DV], U32, TAIL_LANE, 2)

@@ -23,16 +23,17 @@ PASS = P * PACK
 PASSES = SLOTS // PASS
 BLOCKS = D // P
 LAST = BLOCKS - 1
-LIST_COLS = PASS // 16
+LIST_ROWS = 16
 MX_ALIGN = 64
 
-TS_RUN = TOKENS // P
+TS_RUN = TOKENS // (2 * P)
 BANK_COLS = 4
 
+TS_SPLIT = 768
+X_ON_VECTOR = 320
 KIB = 1024
 LANE_KIB = 8
-X_LANE = BLOCKS
-TAIL_LANE = X_LANE + BLOCKS
+H_LANE, DY_LANE, X_LANE = 0, BLOCKS, 2 * BLOCKS
 
 FLOPS = 2 * D * DV * SLOTS
 
@@ -41,257 +42,163 @@ def tile_attend_gex_tnh_w_kernel(tc, xT, dyT, hT, ts, offs, out):
     nc = tc.nc
     with ExitStack() as ctx:
         keep = ctx.enter_context(tc.tile_pool(name="keep", bufs=1))
-        placed = ctx.enter_context(tc.tile_pool(name="placed", bufs=1))
+        lanes = ctx.enter_context(tc.tile_pool(name="lanes", bufs=1))
         psum = ctx.enter_context(tc.psum_pool(name="psum", bufs=1))
 
-        def own(name, shape, dtype):
-            return keep.tile(shape, dtype, name=name, align_bytes=MX_ALIGN)
+        def own(name, shape, dtype, follows=None):
+            return keep.tile(shape, dtype, name=name, tag=follows or name, align_bytes=MX_ALIGN)
 
         def place(name, shape, dtype, lane, kib):
             offset = int((LANE_KIB * lane + kib) * KIB)
-            return placed.tile(shape, dtype, name=name, align_bytes=MX_ALIGN, offset=offset)
+            return lanes.tile(shape, dtype, name=name, align_bytes=MX_ALIGN, offset=offset)
 
         def rows(b):
             return slice(b * P, (b + 1) * P)
 
-        offsets = keep.tile([P, SLOTS // 16], U16, name="offsets")
-        ts_cols = place("ts_cols", [P, TS_RUN], F32, X_LANE, 5)
-        nc.sync.dma_start(ts_cols[:], ts[0, :].rearrange("(p j) -> p j", p=P))
-        pass_lists = [offsets[:, g * LIST_COLS : (g + 1) * LIST_COLS] for g in range(PASSES)]
+        offsets = keep.tile([P, SLOTS // LIST_ROWS], U16, name="offsets")
+
+        def listed(window, slots):
+            return window[:].indirect(offsets[:, slots.start // LIST_ROWS : slots.stop // LIST_ROWS])
+
+        all_slots = slice(0, SLOTS)
         pass_slots = [slice(g * PASS, (g + 1) * PASS) for g in range(PASSES)]
+
+        ts_cols = own("ts_cols", [P, 2, TS_RUN], F32)
+        nc.sync.dma_start(ts_cols[:], ts[0, :].rearrange("(h p j) -> p h j", h=2, p=P))
+
+        nc.sync.dma_start(offsets[:], offs)
 
         ident = keep.tile([P, P], F32, name="ident")
         make_identity(nc, ident[:])
 
-        h_win = [own("h_win%d" % b, [P, TOKENS], F32) for b in range(BLOCKS)]
-        dy_win = [own("dy_win%d" % b, [P, TOKENS], F32) for b in range(BLOCKS)]
-
-        half, quarter = TOKENS // 2, TOKENS // 4
-        x_pieces, x_raw = {}, {}
-        for b in range(LAST):
-            x_pieces[b] = [slice(0, half), slice(half, TOKENS)]
-            x_raw[b, 0] = own("x_raw%d_0" % b, [P, half], F32)
-            if b == 1:
-                x_raw[b, 1] = place("x_raw%d_1" % b, [P, half], F32, b + 1, 4)
-            else:
-                x_raw[b, 1] = own("x_raw%d_1" % b, [P, half], F32)
-        x_pieces[LAST] = [slice(0, half), slice(half, half + quarter), slice(half + quarter, TOKENS)]
-        x_raw[LAST, 0] = place("x_raw_last0", [P, half], F32, TAIL_LANE, 0)
-        x_raw[LAST, 1] = own("x_raw_last1", [P, quarter], F32)
-        x_raw[LAST, 2] = place("x_raw_last2", [P, quarter], F32, TAIL_LANE, 5)
-
-        def load_h(b):
+        h_win = [place("h_win%d" % b, [P, TOKENS], F32, H_LANE + b, 0) for b in range(BLOCKS)]
+        dy_win = [place("dy_win%d" % b, [P, TOKENS], F32, DY_LANE + b, 0) for b in range(BLOCKS)]
+        x_win = [place("x_win%d" % b, [P, TOKENS], F32, X_LANE + b, 0) for b in range(BLOCKS)]
+        for b in range(BLOCKS):
             nc.sync.dma_start(h_win[b][:], hT[rows(b), :])
-
-        def load_dy(b):
             nc.sync.dma_start(dy_win[b][:], dyT[rows(b), :])
-
-        def load_x(b, *pieces):
-            for i in pieces:
-                nc.sync.dma_start(x_raw[b, i][:], xT[rows(b), x_pieces[b][i]])
-
-        for b in range(LAST):
-            load_h(b)
-            if b == 0:
-                nc.sync.dma_start(offsets[:], offs)
-            load_x(b, 0, 1)
-            if b == LAST - 1:
-                load_h(LAST)
-            load_dy(b)
-        load_x(LAST, 0)
-        load_dy(LAST)
-        load_x(LAST, 1, 2)
+        for b in range(BLOCKS):
+            nc.sync.dma_start(x_win[b][:], xT[rows(b), :])
 
         ts_win = own("ts_win", [P, TOKENS], F32)
-        ts_view = ts_win[:].rearrange("m (p j) -> m p j", p=P)
+        ts_view = ts_win[:].rearrange("m (h p j) -> m h p j", h=2, p=P)
         for c in range(TS_RUN // BANK_COLS):
-            spread = psum.tile([P, BANK_COLS, P], F32, name="acc", bufs=BLOCKS)
-            for j in range(BANK_COLS):
-                col = BANK_COLS * c + j
-                nc.tensor.transpose(spread[:, j, :], ts_cols[:, col : col + 1].to_broadcast([P, P]), ident[:])
-            nc.scalar.copy(ts_view[:, :, BANK_COLS * c : BANK_COLS * (c + 1)], spread[:].rearrange("m j p -> m p j"))
+            for half, copy in enumerate((nc.scalar.copy, nc.vector.tensor_copy)):
+                spread = psum.tile([P, BANK_COLS, P], F32, name="acc", bufs=BLOCKS)
+                for j in range(BANK_COLS):
+                    col = BANK_COLS * c + j
+                    nc.tensor.transpose(spread[:, j, :], ts_cols[:, half, col : col + 1].to_broadcast([P, P]), ident[:])
+                copy(ts_view[:, half, :, BANK_COLS * c : BANK_COLS * (c + 1)], spread[:].rearrange("m j p -> m p j"))
+        ts_got = own("ts_got", [P, SLOTS], F32)
+        for slots in (pass_slots[0], slice(PASS, TS_SPLIT)):
+            nc.vector.tensor_copy(ts_got[:, slots], listed(ts_win, slots))
 
-        ts_got = [own("ts_got%d" % g, [P, PASS], F32) for g in range(PASSES)]
+        dz_codes = [own("dz_codes%d" % g, [P, DV], U32) for g in range(PASSES)]
         dz_scales = [own("dz_scales%d" % g, [P, DV], U8) for g in range(PASSES)]
-        dz_banks, dz_turned, dz_codes = {}, {}, {}
-        x_banks, x_turned, x_codes, x_scales = {}, {}, {}, {}
 
-        def gather_h(b, h_got):
-            nc.vector.tensor_copy(h_got[:], h_win[b][:].indirect(offsets[:]))
+        def new_bank(name):
+            return psum.tile([P, PASSES, 2, P], F32, name=name)
 
-        def gather_dy(b, g, dy_ts):
-            nc.vector.tensor_tensor(dy_ts[:], dy_win[b][:].indirect(pass_lists[g]), ts_got[g][:], ALU.mult)
-
-        def square(h_got, squares):
-            for g in range(PASSES):
-                nc.scalar.activation(squares[:, pass_slots[g]], h_got[:, pass_slots[g]], ACT.Square)
-
-        def form_dz(b, g, squares, dy_ts):
-            neg_dz = own("neg_dz%d_%d" % (b, g), [P, PASS], BF16)
-            if b < LAST:
-                nc.vector.scalar_tensor_tensor(
-                    neg_dz[:], squares[:, pass_slots[g]], 1.0, dy_ts[:], ALU.subtract, ALU.mult
-                )
-                pairs = neg_dz[:].bitcast(F32).rearrange("n (p u) -> n u p", u=2)
-            else:
-                laid = neg_dz[:].rearrange("n (u p e) -> n u p e", u=2, e=2)
-                in0 = squares[:, pass_slots[g]].rearrange("n (p u e) -> n u p e", u=2, e=2)
-                in1 = dy_ts[:].rearrange("n (p u e) -> n u p e", u=2, e=2)
-                for u in range(2):
-                    nc.vector.scalar_tensor_tensor(laid[:, u], in0[:, u], 1.0, in1[:, u], ALU.subtract, ALU.mult)
-                pairs = neg_dz[:].bitcast(F32).rearrange("n (u p) -> n u p", u=2)
-            if b < 2:
-                if g == 0:
-                    dz_banks[b, g] = psum.tile([P, PASSES, 2, P], F32, name=("bank_c", "bank_b")[b])
-                bank = dz_banks[b, 0][:, g]
-            else:
-                if b == 2:
-                    dz_banks[b, g] = psum.tile([P, 2, 2, P], F32, name=("bank_a", "bank_b")[g])
-                bank = dz_banks[2, g][:, b - 2]
+        def turn(values, bank):
+            pairs = values.bitcast(F32).rearrange("r (p u) -> r u p", u=2)
             for u in range(2):
                 nc.tensor.transpose(bank[:, u, :], pairs[:, u, :], ident[:])
 
-        def fetch_dz(b, turned):
-            nc.scalar.copy(
-                turned[:].bitcast(F32).rearrange("p (g n u) -> p g n u", g=PASSES, u=2),
-                dz_banks[b, 0][:].rearrange("p g u n -> p g n u"),
+        def fetch(copy, bank, turned):
+            copy(
+                turned[:].bitcast(F32).rearrange("p (g r u) -> p g r u", g=PASSES, u=2),
+                bank[:].rearrange("p g u r -> p g r u"),
             )
+
+        def quantize_dz(b, turned):
             for g in range(PASSES):
-                dz_turned[b, g] = turned[:, pass_slots[g]]
+                codes = dz_codes[g][:, rows(b)].bitcast(E5M2)
+                nc.vector.quantize_mx(out=codes, scales=dz_scales[g][:, rows(b)], in_=turned[:, pass_slots[g]])
 
-        def quantize_dz(b, g):
-            codes = dz_codes[g][:, rows(b)].bitcast(E5M2)
-            nc.vector.quantize_mx(out=codes, scales=dz_scales[g][:, rows(b)], in_=dz_turned[b, g])
-
-        def close_pass(g, turned):
-            nc.scalar.copy(
-                turned[:].bitcast(F32).rearrange("p (b n u) -> p b n u", b=2, u=2),
-                dz_banks[2, g][:].rearrange("p b u n -> p b n u"),
-            )
-            cols = slice(2 * P, 4 * P)
-            nc.vector.quantize_mx(out=dz_codes[g][:, cols].bitcast(E5M2), scales=dz_scales[g][:, cols], in_=turned[:])
-
-        def cast_x(b, x_win):
-            for i, piece in enumerate(x_pieces[b]):
-                nc.scalar.activation(x_win[:, piece], x_raw[b, i][:], ACT.Copy)
-
-        def gather_x(b, x_win, x_got):
-            laid = x_got[:].rearrange("d (u r e) -> d r u e", u=2, e=2)
-            nc.scalar.activation(laid, x_win[:].indirect(offsets[:]), ACT.Copy)
-            pairs = x_got[:].bitcast(F32).rearrange("d (u g p) -> d g u p", g=PASSES, u=2)
-            x_banks[b] = psum.tile([P, PASSES, 2, P], F32, name=("bank_c", "bank_d")[b % 2])
-            for g in range(PASSES):
-                for u in range(2):
-                    nc.tensor.transpose(x_banks[b][:, g, u, :], pairs[:, g, u, :], ident[:])
-
-        def fetch_x(b, turned):
-            x_turned[b] = turned
-            nc.scalar.copy(
-                turned[:].bitcast(F32).rearrange("p (g d u) -> p g d u", g=PASSES, u=2),
-                x_banks[b][:].rearrange("p g u d -> p g d u"),
-            )
+        bank = None
+        for b in range(BLOCKS):
+            h_got = own("h_got%d" % b, [P, SLOTS], F32, "ts_cols")
+            for slots in pass_slots:
+                nc.scalar.activation(h_got[:, slots], listed(h_win[b], slots), ACT.Copy)
+            if b == 0:
+                rest = slice(TS_SPLIT, SLOTS)
+                nc.scalar.activation(ts_got[:, rest], listed(ts_win, rest), ACT.Copy)
+            dy_ts = own("dy_ts%d" % b, [P, SLOTS], F32, "dy_ts")
+            for slots in pass_slots:
+                nc.vector.tensor_tensor(dy_ts[:, slots], listed(dy_win[b], slots), ts_got[:, slots], ALU.mult)
+            if b == 0:
+                squares = own("squares0", [P, SLOTS], F32, "ts_win")
+            else:
+                squares = place("squares%d" % b, [P, SLOTS], F32, H_LANE + b - 1, 0)
+            for slots in pass_slots:
+                nc.scalar.activation(squares[:, slots], h_got[:, slots], ACT.Square)
+            if b > 0:
+                turned = place("dz_turned%d" % (b - 1), [P, SLOTS], BF16, H_LANE + b, 4)
+                fetch(nc.scalar.copy, bank, turned)
+            bank = new_bank("bank_%s" % "ab"[b % 2])
+            for g, slots in enumerate(pass_slots):
+                neg_dz = place("neg_dz%d_%d" % (b, g), [P, PASS], BF16, H_LANE + b, 2 * g)
+                nc.vector.scalar_tensor_tensor(neg_dz[:], squares[:, slots], 1.0, dy_ts[:, slots], ALU.subtract, ALU.mult)
+                turn(neg_dz[:], bank[:, g])
+            if b > 0:
+                quantize_dz(b - 1, turned)
 
         x_width = PASSES * P
+        x_banks, x_turned, x_codes, x_scales = {}, {}, {}, {}
 
-        def quantize_x(b, codes, scales):
-            x_codes[b], x_scales[b] = codes, scales
-            nc.vector.quantize_mx(out=codes[:].bitcast(E4M3), scales=scales[:], in_=x_turned[b][:])
+        def gather_x(b, x_got, on_vector):
+            if on_vector:
+                first = slice(0, on_vector)
+                nc.vector.tensor_copy(x_got[:, first], listed(x_win[b], first))
+            rest = slice(on_vector, SLOTS)
+            nc.scalar.activation(x_got[:, rest], listed(x_win[b], rest), ACT.Copy)
+            x_banks[b] = new_bank("bank_%s" % "cd"[b % 2])
+            for g in range(PASSES):
+                turn(x_got[:, pass_slots[g]], x_banks[b][:, g])
+
+        def fetch_x(b, copy, turned):
+            x_turned[b] = turned
+            fetch(copy, x_banks[b], turned)
+
+        def quantize_x(b, codes):
+            x_codes[b] = codes
+            x_scales[b] = own("x_scales%d" % b, [P, x_width], U8)
+            nc.vector.quantize_mx(out=codes[:].bitcast(E4M3), scales=x_scales[b][:], in_=x_turned[b][:])
 
         accs = [psum.tile([P, DV], F32, name="acc", bufs=BLOCKS) for b in range(BLOCKS)]
 
-        def multiply(b, g):
-            nc.tensor.matmul_mx(
-                out=accs[b][:],
-                lhsT=x_codes[b][:, rows(g)].bitcast(E4M3),
-                lhsT_scale=x_scales[b][:, rows(g)],
-                rhs=dz_codes[g][:].bitcast(E5M2),
-                rhs_scale=dz_scales[g][:],
-                start=(g == 0),
-                stop=(g == PASSES - 1),
-            )
-
-        def store(b):
-            pieces = 2 if b == LAST else 1
-            for i in range(pieces):
-                cols = slice(i * DV // pieces, (i + 1) * DV // pieces)
-                result = own("result%d_%d" % (b, i), [P, DV // pieces], F32)
-                if b % 2 == 0:
-                    nc.scalar.activation(result[:], accs[b][:, cols], ACT.Copy, scale=-1.0)
-                else:
-                    nc.vector.tensor_scalar_mul(result[:], accs[b][:, cols], -1.0)
-                nc.sync.dma_start(out[0, rows(b), cols], result[:])
-
-        for b in range(LAST):
-            x_win = place("x_win%d" % b, [P, TOKENS], BF16, X_LANE + b, 2)
-            cast_x(b, x_win)
-            if b == 2:
-                fetch_x(b - 1, own("x_raw%d_0" % b, [P, SLOTS], BF16))
-
-            if b == 0:
-                h_got = own("h_got0", [P, SLOTS], F32)
-            else:
-                h_got = place("h_got%d" % b, [P, SLOTS], F32, b - 1, 1)
-            gather_h(b, h_got)
-            if b == 0:
-                for g in range(PASSES):
-                    nc.vector.tensor_copy(ts_got[g][:], ts_win[:].indirect(pass_lists[g]))
-            if b == 2:
-                quantize_x(0, place("x_codes0", [P, x_width], U32, 1, 5), own("x_scales0", [P, x_width], U8))
-
-            gather_x(b, x_win, place("x_got%d" % b, [P, SLOTS], BF16, X_LANE + b + 1, 5))
-            if b == 2:
-                squares = place("squares%d" % b, [P, SLOTS], F32, TAIL_LANE, 17)
-            else:
-                squares = place("squares%d" % b, [P, SLOTS], F32, b + 1, 4)
-            if b == 1:
-                square(h_got, squares)
-            else:
-                nc.gpsimd.tensor_tensor(squares[:], h_got[:], h_got[:], ALU.mult)
-            if b == 0:
-                fetch_x(b, place("x_turned0", [P, SLOTS], BF16, TAIL_LANE, 16))
-            else:
-                fetch_dz(b - 1, place("dz_turned%d" % (b - 1), [P, SLOTS], BF16, X_LANE + b, 2))
-            if b == 2:
-                fetch_x(b, own("x_turned2", [P, SLOTS], BF16))
-                last_h = own("h_got%d" % LAST, [P, SLOTS], F32)
-                gather_h(LAST, last_h)
-                last_squares = own("squares%d" % LAST, [P, SLOTS], F32)
-                square(last_h, last_squares)
-
-            dy_ts = [place("dy_ts%d_%d" % (b, g), [P, PASS], F32, b, 4 + 2 * g) for g in range(PASSES)]
+        def multiply(b):
             for g in range(PASSES):
-                gather_dy(b, g, dy_ts[g])
-            for g in range(PASSES):
-                form_dz(b, g, squares, dy_ts[g])
+                nc.tensor.matmul_mx(
+                    out=accs[b][:],
+                    lhsT=x_codes[b][:, rows(g)].bitcast(E4M3),
+                    lhsT_scale=x_scales[b][:, rows(g)],
+                    rhs=dz_codes[g][:].bitcast(E5M2),
+                    rhs_scale=dz_scales[g][:],
+                    start=(g == 0),
+                    stop=(g == PASSES - 1),
+                )
 
-        x_win = place("x_win%d" % LAST, [P, TOKENS], BF16, X_LANE + LAST, 2)
-        cast_x(LAST, x_win)
-        dy_ts = [place("dy_ts3_%d" % g, [P, PASS], F32, TAIL_LANE, 19 - 2 * g) for g in range(PASSES)]
-        for g in range(PASSES):
-            gather_dy(LAST, g, dy_ts[g])
-        gather_x(LAST, x_win, own("x_got%d" % LAST, [P, SLOTS], BF16))
+        def store(b, on_vector, result):
+            if on_vector:
+                nc.vector.tensor_scalar_mul(result[:], accs[b][:], -1.0)
+            else:
+                nc.scalar.activation(result[:], accs[b][:], ACT.Copy, scale=-1.0)
+            nc.sync.dma_start(out[0, rows(b), :], result[:])
 
-        for g in range(PASSES):
-            form_dz(LAST, g, last_squares, dy_ts[g])
-
-        dz_codes[0] = place("dz_codes0", [P, DV], U32, TAIL_LANE, 20)
+        gather_x(0, own("x_got0", [P, SLOTS], BF16, "ts_cols"), 0)
+        turned = own("dz_turned3", [P, SLOTS], BF16)
+        fetch(nc.vector.tensor_copy, bank, turned)
+        quantize_dz(LAST, turned)
+        for b in range(1, BLOCKS):
+            gather_x(b, own("x_got%d" % b, [P, SLOTS], BF16), X_ON_VECTOR)
+            fetch_x(b - 1, nc.vector.tensor_copy, place("x_turned%d" % (b - 1), [P, SLOTS], BF16, X_LANE + b, 0))
+            quantize_x(b - 1, own("x_codes%d" % (b - 1), [P, x_width], U32))
+            multiply(b - 1)
         for b in range(2):
-            quantize_dz(b, 0)
-        quantize_x(1, own("x_codes1", [P, x_width], U32), place("x_scales1", [P, x_width], U8, TAIL_LANE, 19))
-
-        close_pass(0, place("dz_late0", [P, SLOTS], BF16, TAIL_LANE, 3.5))
-        dz_codes[1] = place("dz_codes1", [P, DV], U32, TAIL_LANE, 2)
-        for b in range(2):
-            quantize_dz(b, 1)
-        close_pass(1, place("dz_late1", [P, SLOTS], BF16, TAIL_LANE, 6))
-        quantize_x(2, own("x_codes2", [P, x_width], U32), place("x_scales2", [P, x_width], U8, TAIL_LANE, 6))
-        fetch_x(LAST, own("x_turned3", [P, SLOTS], BF16))
-        quantize_x(LAST, own("x_codes3", [P, x_width], U32), own("x_scales3", [P, x_width], U8))
-
-        multiply(0, 0)
-        multiply(1, 0)
-        for b in range(BLOCKS):
-            if b > 1:
-                multiply(b, 0)
-            multiply(b, 1)
-            store(b)
+            store(b, False, place("result%d" % b, [P, DV], F32, X_LANE + LAST, 2 + 2 * b))
+        fetch_x(3, nc.scalar.copy, own("x_turned3", [P, SLOTS], BF16))
+        quantize_x(3, own("x_codes3", [P, x_width], U32))
+        store(2, False, own("result2", [P, DV], F32))
+        multiply(3)
+        store(3, True, own("result3", [P, DV], F32))

@@ -30,7 +30,7 @@ TS_RUN = TOKENS // (2 * P)
 BANK_COLS = 4
 
 TS_SPLIT = 768
-X_ON_VECTOR = 320
+X_ON_VECTOR = 384
 KIB = 1024
 LANE_KIB = 8
 H_LANE, DY_LANE, X_LANE = 0, BLOCKS, 2 * BLOCKS
@@ -96,9 +96,6 @@ def tile_attend_gex_tnh_w_kernel(tc, xT, dyT, hT, ts, offs, out):
         dz_codes = [own("dz_codes%d" % g, [P, DV], U32) for g in range(PASSES)]
         dz_scales = [own("dz_scales%d" % g, [P, DV], U8) for g in range(PASSES)]
 
-        def new_bank(name):
-            return psum.tile([P, PASSES, 2, P], F32, name=name)
-
         def turn(values, bank):
             pairs = values.bitcast(F32).rearrange("r (p u) -> r u p", u=2)
             for u in range(2):
@@ -110,10 +107,12 @@ def tile_attend_gex_tnh_w_kernel(tc, xT, dyT, hT, ts, offs, out):
                 bank[:].rearrange("p g u r -> p g r u"),
             )
 
-        def quantize_dz(b, turned):
-            for g in range(PASSES):
-                codes = dz_codes[g][:, rows(b)].bitcast(E5M2)
-                nc.vector.quantize_mx(out=codes, scales=dz_scales[g][:, rows(b)], in_=turned[:, pass_slots[g]])
+        def fetch_pass(copy, bank, turned):
+            copy(turned[:].bitcast(F32).rearrange("p (r u) -> p r u", u=2), bank[:].rearrange("p u r -> p r u"))
+
+        def quantize_dz(b, g, turned):
+            codes = dz_codes[g][:, rows(b)].bitcast(E5M2)
+            nc.vector.quantize_mx(out=codes, scales=dz_scales[g][:, rows(b)], in_=turned)
 
         bank = None
         for b in range(BLOCKS):
@@ -135,16 +134,21 @@ def tile_attend_gex_tnh_w_kernel(tc, xT, dyT, hT, ts, offs, out):
             if b > 0:
                 turned = place("dz_turned%d" % (b - 1), [P, SLOTS], BF16, H_LANE + b, 4)
                 fetch(nc.scalar.copy, bank, turned)
-            bank = new_bank("bank_%s" % "ab"[b % 2])
+            if b < LAST:
+                bank = psum.tile([P, PASSES, 2, P], F32, name="bank_%s" % "ab"[b % 2])
+                banks = [bank[:, g] for g in range(PASSES)]
+            else:
+                banks = [psum.tile([P, 2, P], F32, name="bank_%s" % "bc"[g]) for g in range(PASSES)]
             for g, slots in enumerate(pass_slots):
                 neg_dz = place("neg_dz%d_%d" % (b, g), [P, PASS], BF16, H_LANE + b, 2 * g)
                 nc.vector.scalar_tensor_tensor(neg_dz[:], squares[:, slots], 1.0, dy_ts[:, slots], ALU.subtract, ALU.mult)
-                turn(neg_dz[:], bank[:, g])
+                turn(neg_dz[:], banks[g])
             if b > 0:
-                quantize_dz(b - 1, turned)
+                for g, slots in enumerate(pass_slots):
+                    quantize_dz(b - 1, g, turned[:, slots])
 
         x_width = PASSES * P
-        x_banks, x_turned, x_codes, x_scales = {}, {}, {}, {}
+        x_banks, x_codes, x_scales = {}, {}, {}
 
         def gather_x(b, x_got, on_vector):
             if on_vector:
@@ -152,53 +156,58 @@ def tile_attend_gex_tnh_w_kernel(tc, xT, dyT, hT, ts, offs, out):
                 nc.vector.tensor_copy(x_got[:, first], listed(x_win[b], first))
             rest = slice(on_vector, SLOTS)
             nc.scalar.activation(x_got[:, rest], listed(x_win[b], rest), ACT.Copy)
-            x_banks[b] = new_bank("bank_%s" % "cd"[b % 2])
             for g in range(PASSES):
-                turn(x_got[:, pass_slots[g]], x_banks[b][:, g])
+                x_banks[b, g] = psum.tile([P, 2, P], F32, name="bank_%s" % ("da", "bc")[b % 2][g])
+                turn(x_got[:, pass_slots[g]], x_banks[b, g])
 
-        def fetch_x(b, copy, turned):
-            x_turned[b] = turned
-            fetch(copy, x_banks[b], turned)
-
-        def quantize_x(b, codes):
-            x_codes[b] = codes
+        def quantize_x(b, copies, turned):
+            for g in range(PASSES):
+                fetch_pass(copies[g], x_banks[b, g], turned[g])
+            x_codes[b] = own("x_codes%d" % b, [P, x_width], U32)
             x_scales[b] = own("x_scales%d" % b, [P, x_width], U8)
-            nc.vector.quantize_mx(out=codes[:].bitcast(E4M3), scales=x_scales[b][:], in_=x_turned[b][:])
+            for g in range(PASSES):
+                codes = x_codes[b][:, rows(g)].bitcast(E4M3)
+                nc.vector.quantize_mx(out=codes, scales=x_scales[b][:, rows(g)], in_=turned[g][:])
 
-        accs = [psum.tile([P, DV], F32, name="acc", bufs=BLOCKS) for b in range(BLOCKS)]
-
-        def multiply(b):
+        def multiply(b, acc, cols):
             for g in range(PASSES):
                 nc.tensor.matmul_mx(
-                    out=accs[b][:],
+                    out=acc[:],
                     lhsT=x_codes[b][:, rows(g)].bitcast(E4M3),
                     lhsT_scale=x_scales[b][:, rows(g)],
-                    rhs=dz_codes[g][:].bitcast(E5M2),
-                    rhs_scale=dz_scales[g][:],
+                    rhs=dz_codes[g][:, cols].bitcast(E5M2),
+                    rhs_scale=dz_scales[g][:, cols],
                     start=(g == 0),
                     stop=(g == PASSES - 1),
                 )
 
-        def store(b, on_vector, result):
+        def store(b, acc, cols, on_vector, result):
             if on_vector:
-                nc.vector.tensor_scalar_mul(result[:], accs[b][:], -1.0)
+                nc.vector.tensor_scalar_mul(result[:], acc[:], -1.0)
             else:
-                nc.scalar.activation(result[:], accs[b][:], ACT.Copy, scale=-1.0)
-            nc.sync.dma_start(out[0, rows(b), :], result[:])
+                nc.scalar.activation(result[:], acc[:], ACT.Copy, scale=-1.0)
+            nc.sync.dma_start(out[0, rows(b), cols], result[:])
 
         gather_x(0, own("x_got0", [P, SLOTS], BF16, "ts_cols"), 0)
-        turned = own("dz_turned3", [P, SLOTS], BF16)
-        fetch(nc.vector.tensor_copy, bank, turned)
-        quantize_dz(LAST, turned)
+        turned = [own("dz_turned3_%d" % g, [P, PASS], BF16) for g in range(PASSES)]
+        for g in range(PASSES):
+            fetch_pass(nc.vector.tensor_copy, banks[g], turned[g])
+        for g in range(PASSES):
+            quantize_dz(LAST, g, turned[g][:])
+        all_cols = slice(0, DV)
+        accs = [psum.tile([P, DV], F32, name="acc", bufs=BLOCKS) for b in range(LAST)]
         for b in range(1, BLOCKS):
             gather_x(b, own("x_got%d" % b, [P, SLOTS], BF16), X_ON_VECTOR)
-            fetch_x(b - 1, nc.vector.tensor_copy, place("x_turned%d" % (b - 1), [P, SLOTS], BF16, X_LANE + b, 0))
-            quantize_x(b - 1, own("x_codes%d" % (b - 1), [P, x_width], U32))
-            multiply(b - 1)
-        for b in range(2):
-            store(b, False, place("result%d" % b, [P, DV], F32, X_LANE + LAST, 2 + 2 * b))
-        fetch_x(3, nc.scalar.copy, own("x_turned3", [P, SLOTS], BF16))
-        quantize_x(3, own("x_codes3", [P, x_width], U32))
-        store(2, False, own("result2", [P, DV], F32))
-        multiply(3)
-        store(3, True, own("result3", [P, DV], F32))
+            turned = [place("x_turned%d_%d" % (b - 1, g), [P, PASS], BF16, X_LANE + b, 5 * g) for g in range(PASSES)]
+            quantize_x(b - 1, (nc.vector.tensor_copy, nc.scalar.copy), turned)
+            multiply(b - 1, accs[b - 1], all_cols)
+        turned = [own("x_turned3_%d" % g, [P, PASS], BF16) for g in range(PASSES)]
+        quantize_x(LAST, (nc.scalar.copy, nc.scalar.copy), turned)
+        store(0, accs[0], all_cols, False, place("result0", [P, DV], F32, X_LANE + LAST, 2))
+        store(1, accs[1], all_cols, True, place("result1", [P, DV], F32, X_LANE + LAST, 4))
+        store(2, accs[2], all_cols, False, own("result2", [P, DV], F32))
+        halves = [slice(0, DV // 2), slice(DV // 2, DV)]
+        last_accs = [psum.tile([P, DV // 2], F32, name="acc", bufs=BLOCKS), psum.tile([P, DV // 2], F32, name="bank_d")]
+        for i, cols in enumerate(halves):
+            multiply(LAST, last_accs[i], cols)
+            store(LAST, last_accs[i], cols, i == 1, own("result3_%d" % i, [P, DV // 2], F32))

from contextlib import ExitStack

import concourse.mybir as mybir
from concourse.masks import make_identity

F32 = mybir.dt.float32
BF16 = mybir.dt.bfloat16
U32 = mybir.dt.uint32
U16 = mybir.dt.uint16
U8 = mybir.dt.uint8
E4M3 = mybir.dt.float8_e4m3fn_x4
E5M2 = mybir.dt.float8_e5m2_x4
ACT = mybir.ActivationFunctionType
ALU = mybir.AluOpType

P = 128
TOKENS = 2048
SLOTS = 1024
D = 512
DV = 512
PACK = 4
PASS = P * PACK
PASSES = SLOTS // PASS
BLOCKS = D // P
LAST = BLOCKS - 1
LIST_ROWS = 16
MX_ALIGN = 64

TS_RUN = TOKENS // (2 * P)
BANK_COLS = 4

TS_SPLIT = 768
X_ON_VECTOR = 384
KIB = 1024
LANE_KIB = 8
H_LANE, DY_LANE, X_LANE = 0, BLOCKS, 2 * BLOCKS

FLOPS = 2 * D * DV * SLOTS


def tile_attend_gex_tnh_w_kernel(tc, xT, dyT, hT, ts, offs, out):
    nc = tc.nc
    with ExitStack() as ctx:
        keep = ctx.enter_context(tc.tile_pool(name="keep", bufs=1))
        lanes = ctx.enter_context(tc.tile_pool(name="lanes", bufs=1))
        psum = ctx.enter_context(tc.psum_pool(name="psum", bufs=1))

        def own(name, shape, dtype, follows=None):
            return keep.tile(shape, dtype, name=name, tag=follows or name, align_bytes=MX_ALIGN)

        def place(name, shape, dtype, lane, kib):
            offset = int((LANE_KIB * lane + kib) * KIB)
            return lanes.tile(shape, dtype, name=name, align_bytes=MX_ALIGN, offset=offset)

        def rows(b):
            return slice(b * P, (b + 1) * P)

        offsets = keep.tile([P, SLOTS // LIST_ROWS], U16, name="offsets")

        def listed(window, slots):
            return window[:].indirect(offsets[:, slots.start // LIST_ROWS : slots.stop // LIST_ROWS])

        all_slots = slice(0, SLOTS)
        pass_slots = [slice(g * PASS, (g + 1) * PASS) for g in range(PASSES)]

        ts_cols = own("ts_cols", [P, 2, TS_RUN], F32)
        nc.sync.dma_start(ts_cols[:], ts[0, :].rearrange("(h p j) -> p h j", h=2, p=P))

        nc.sync.dma_start(offsets[:], offs)

        ident = keep.tile([P, P], F32, name="ident")
        make_identity(nc, ident[:])

        h_win = [place("h_win%d" % b, [P, TOKENS], F32, H_LANE + b, 0) for b in range(BLOCKS)]
        dy_win = [place("dy_win%d" % b, [P, TOKENS], F32, DY_LANE + b, 0) for b in range(BLOCKS)]
        x_win = [place("x_win%d" % b, [P, TOKENS], F32, X_LANE + b, 0) for b in range(BLOCKS)]
        for b in range(BLOCKS):
            nc.sync.dma_start(h_win[b][:], hT[rows(b), :])
            nc.sync.dma_start(dy_win[b][:], dyT[rows(b), :])
        for b in range(BLOCKS):
            nc.sync.dma_start(x_win[b][:], xT[rows(b), :])

        ts_win = own("ts_win", [P, TOKENS], F32)
        ts_view = ts_win[:].rearrange("m (h p j) -> m h p j", h=2, p=P)
        for c in range(TS_RUN // BANK_COLS):
            for half, copy in enumerate((nc.scalar.copy, nc.vector.tensor_copy)):
                spread = psum.tile([P, BANK_COLS, P], F32, name="acc", bufs=BLOCKS)
                for j in range(BANK_COLS):
                    col = BANK_COLS * c + j
                    nc.tensor.transpose(spread[:, j, :], ts_cols[:, half, col : col + 1].to_broadcast([P, P]), ident[:])
                copy(ts_view[:, half, :, BANK_COLS * c : BANK_COLS * (c + 1)], spread[:].rearrange("m j p -> m p j"))
        ts_got = own("ts_got", [P, SLOTS], F32)
        for slots in (pass_slots[0], slice(PASS, TS_SPLIT)):
            nc.vector.tensor_copy(ts_got[:, slots], listed(ts_win, slots))

        dz_codes = [own("dz_codes%d" % g, [P, DV], U32) for g in range(PASSES)]
        dz_scales = [own("dz_scales%d" % g, [P, DV], U8) for g in range(PASSES)]

        def turn(values, bank):
            pairs = values.bitcast(F32).rearrange("r (p u) -> r u p", u=2)
            for u in range(2):
                nc.tensor.transpose(bank[:, u, :], pairs[:, u, :], ident[:])

        def fetch(copy, bank, turned):
            copy(
                turned[:].bitcast(F32).rearrange("p (g r u) -> p g r u", g=PASSES, u=2),
                bank[:].rearrange("p g u r -> p g r u"),
            )

        def fetch_pass(copy, bank, turned):
            copy(turned[:].bitcast(F32).rearrange("p (r u) -> p r u", u=2), bank[:].rearrange("p u r -> p r u"))

        def quantize_dz(b, g, turned):
            codes = dz_codes[g][:, rows(b)].bitcast(E5M2)
            nc.vector.quantize_mx(out=codes, scales=dz_scales[g][:, rows(b)], in_=turned)

        bank = None
        for b in range(BLOCKS):
            h_got = own("h_got%d" % b, [P, SLOTS], F32, "ts_cols")
            for slots in pass_slots:
                nc.scalar.activation(h_got[:, slots], listed(h_win[b], slots), ACT.Copy)
            if b == 0:
                rest = slice(TS_SPLIT, SLOTS)
                nc.scalar.activation(ts_got[:, rest], listed(ts_win, rest), ACT.Copy)
            dy_ts = own("dy_ts%d" % b, [P, SLOTS], F32, "dy_ts")
            for slots in pass_slots:
                nc.vector.tensor_tensor(dy_ts[:, slots], listed(dy_win[b], slots), ts_got[:, slots], ALU.mult)
            if b == 0:
                squares = own("squares0", [P, SLOTS], F32, "ts_win")
            else:
                squares = place("squares%d" % b, [P, SLOTS], F32, H_LANE + b - 1, 0)
            for slots in pass_slots:
                nc.scalar.activation(squares[:, slots], h_got[:, slots], ACT.Square)
            if b > 0:
                turned = place("dz_turned%d" % (b - 1), [P, SLOTS], BF16, H_LANE + b, 4)
                fetch(nc.scalar.copy, bank, turned)
            if b < LAST:
                bank = psum.tile([P, PASSES, 2, P], F32, name="bank_%s" % "ab"[b % 2])
                banks = [bank[:, g] for g in range(PASSES)]
            else:
                banks = [psum.tile([P, 2, P], F32, name="bank_%s" % "bc"[g]) for g in range(PASSES)]
            for g, slots in enumerate(pass_slots):
                neg_dz = place("neg_dz%d_%d" % (b, g), [P, PASS], BF16, H_LANE + b, 2 * g)
                nc.vector.scalar_tensor_tensor(neg_dz[:], squares[:, slots], 1.0, dy_ts[:, slots], ALU.subtract, ALU.mult)
                turn(neg_dz[:], banks[g])
            if b > 0:
                for g, slots in enumerate(pass_slots):
                    quantize_dz(b - 1, g, turned[:, slots])

        x_width = PASSES * P
        x_banks, x_codes, x_scales = {}, {}, {}

        def gather_x(b, x_got, on_vector):
            if on_vector:
                first = slice(0, on_vector)
                nc.vector.tensor_copy(x_got[:, first], listed(x_win[b], first))
            rest = slice(on_vector, SLOTS)
            nc.scalar.activation(x_got[:, rest], listed(x_win[b], rest), ACT.Copy)
            for g in range(PASSES):
                x_banks[b, g] = psum.tile([P, 2, P], F32, name="bank_%s" % ("da", "bc")[b % 2][g])
                turn(x_got[:, pass_slots[g]], x_banks[b, g])

        def quantize_x(b, copies, turned):
            for g in range(PASSES):
                fetch_pass(copies[g], x_banks[b, g], turned[g])
            x_codes[b] = own("x_codes%d" % b, [P, x_width], U32)
            x_scales[b] = own("x_scales%d" % b, [P, x_width], U8)
            for g in range(PASSES):
                codes = x_codes[b][:, rows(g)].bitcast(E4M3)
                nc.vector.quantize_mx(out=codes, scales=x_scales[b][:, rows(g)], in_=turned[g][:])

        def multiply(b, acc, cols):
            for g in range(PASSES):
                nc.tensor.matmul_mx(
                    out=acc[:],
                    lhsT=x_codes[b][:, rows(g)].bitcast(E4M3),
                    lhsT_scale=x_scales[b][:, rows(g)],
                    rhs=dz_codes[g][:, cols].bitcast(E5M2),
                    rhs_scale=dz_scales[g][:, cols],
                    start=(g == 0),
                    stop=(g == PASSES - 1),
                )

        def store(b, acc, cols, on_vector, result):
            if on_vector:
                nc.vector.tensor_scalar_mul(result[:], acc[:], -1.0)
            else:
                nc.scalar.activation(result[:], acc[:], ACT.Copy, scale=-1.0)
            nc.sync.dma_start(out[0, rows(b), cols], result[:])

        gather_x(0, own("x_got0", [P, SLOTS], BF16, "ts_cols"), 0)
        turned = [own("dz_turned3_%d" % g, [P, PASS], BF16) for g in range(PASSES)]
        for g in range(PASSES):
            fetch_pass(nc.vector.tensor_copy, banks[g], turned[g])
        for g in range(PASSES):
            quantize_dz(LAST, g, turned[g][:])
        all_cols = slice(0, DV)
        accs = [psum.tile([P, DV], F32, name="acc", bufs=BLOCKS) for b in range(LAST)]
        for b in range(1, BLOCKS):
            gather_x(b, own("x_got%d" % b, [P, SLOTS], BF16), X_ON_VECTOR)
            turned = [place("x_turned%d_%d" % (b - 1, g), [P, PASS], BF16, X_LANE + b, 5 * g) for g in range(PASSES)]
            quantize_x(b - 1, (nc.vector.tensor_copy, nc.scalar.copy), turned)
            multiply(b - 1, accs[b - 1], all_cols)
        turned = [own("x_turned3_%d" % g, [P, PASS], BF16) for g in range(PASSES)]
        quantize_x(LAST, (nc.scalar.copy, nc.scalar.copy), turned)
        store(0, accs[0], all_cols, False, place("result0", [P, DV], F32, X_LANE + LAST, 2))
        store(1, accs[1], all_cols, True, place("result1", [P, DV], F32, X_LANE + LAST, 4))
        store(2, accs[2], all_cols, False, own("result2", [P, DV], F32))
        halves = [slice(0, DV // 2), slice(DV // 2, DV)]
        last_accs = [psum.tile([P, DV // 2], F32, name="acc", bufs=BLOCKS), psum.tile([P, DV // 2], F32, name="bank_d")]
        for i, cols in enumerate(halves):
            multiply(LAST, last_accs[i], cols)
            store(LAST, last_accs[i], cols, i == 1, own("result3_%d" % i, [P, DV // 2], F32))
